import numpy as np, ml_dtypes
CORES = [24,25,26,27,28,29,30,31]
N = 8
BF = ml_dtypes.bfloat16
def gentries(a):
    return np.ascontiguousarray(a.reshape(8, 16, -1).transpose(0, 2, 1)).reshape(8, -1)
def gtable(e):
    e = np.asarray(e); return np.ascontiguousarray(e.reshape(8, -1, 16).transpose(0, 2, 1)).reshape(128, -1).astype(np.int32)
W, L, K, CAP, NEED, RO = 4096, 256, 3, 96, 8, 3
def take(a, i):
    return np.take_along_axis(a, i.reshape(N, 8, -1), 2).reshape(i.shape)
def shade(rng, h):
    return np.clip(h[:, :, None, :] + rng.integers(-40, 41, (N, 8, 16, h.shape[2])), 0, 255)
def parts(rng):
    h = rng.integers(0, 256, (N, 8, W)); X = shade(rng, h); A = shade(rng, rng.integers(0, 256, (N, 8, L)))
    F = W // 32; pc = np.argsort(rng.random((N, 8, W)), axis=-1); fam = np.argsort(pc, axis=-1) // 32
    first = take(rng.integers(0, W, (N, 8, F)), fam)[:, :, None, :]; size = take(rng.choice(np.array([6, 12, 24, 96]), (N, 8, F)), fam)[:, :, None, :]
    I = take(np.argsort(h, axis=-1), (first + (rng.random((N, 8, 16, W)) * size).astype(np.int64)) % W)
    I = np.where(rng.random((N, 8, 16, W)) < 0.25, rng.integers(0, W, (N, 8, 16, W)), I)
    O = take(pc, 32 * rng.integers(0, F, (N, 8, 1, W)) + rng.integers(0, 32, (N, 8, K, W)))
    mixed = (rng.random((N, 8, 1, W)) < 0.4) | (rng.random((N, 8, K, W)) < 0.1)
    O = np.where(mixed, rng.integers(0, W, (N, 8, K, W)), O)
    return I, X, O, rng.integers(0, W, (N, 8, L)), A, rng.integers(600, 2000, (N, 8, RO))
def pack(I, X, O, g, A, T):
    return {"icol": np.ascontiguousarray(I.reshape(N, 128, W)).astype(np.int32), "pat": np.ascontiguousarray(X.reshape(N, 128, W)).astype(np.float32).astype(BF),
            "alt": np.ascontiguousarray(O.reshape(N, 8 * K, W)).astype(np.int32), "gate": np.stack([gtable(a) for a in g]),
            "acc0": np.ascontiguousarray(A.reshape(N, 128, L)).astype(np.float32).astype(BF), "th": np.ascontiguousarray(T).astype(np.int32)}
def setup_inputs(rng):
    return pack(*parts(rng))
def setup_inputs_spread(rng):
    I, X, O, g, A, T = parts(rng)
    X = np.minimum((np.exp2(8 * rng.random((N, 8, 1, W))) * rng.random((N, 8, 16, W))).astype(np.int64), 255)
    A = np.minimum((np.exp2(8 * rng.random((N, 8, 1, L))) * rng.random((N, 8, 16, L))).astype(np.int64), 255)
    I = np.minimum((W * rng.random((N, 8, 16, W)) ** rng.choice(np.array([1.0, 2.0, 4.0]), (N, 8, 1, W))).astype(np.int64), W - 1)
    O = np.minimum((W * rng.random((N, 8, K, W)) ** rng.choice(np.array([1.0, 2.0, 4.0]), (N, 8, 1, W))).astype(np.int64), W - 1)
    I[:, 1::2] = W - 1 - I[:, 1::2]; O[:, 2::4] = W - 1 - O[:, 2::4]
    T = np.minimum(np.exp2(5 + 7 * rng.random((N, 8, RO))).astype(np.int64), 4080)
    return pack(I, X, O, g, A, T)
def setup_inputs_ends(rng):
    e = np.array([0, W - 1])
    I = np.where(rng.random((N, 8, 1, W)) < 0.25, rng.integers(0, W, (N, 8, 16, W)), e[rng.integers(0, 2, (N, 8, 16, W))])
    O = np.where(rng.random((N, 8, K, W)) < 0.3, rng.integers(0, W, (N, 8, K, W)), e[rng.integers(0, 2, (N, 8, K, W))])
    g = np.where(rng.random((N, 8, L)) < 0.3, rng.integers(0, W, (N, 8, L)), e[rng.integers(0, 2, (N, 8, L))])
    X = 255 * np.where(rng.random((N, 8, 1, W)) < 0.5, rng.integers(0, 2, (N, 8, 1, W)), rng.integers(0, 2, (N, 8, 16, W)))
    A = 255 * np.where(rng.random((N, 8, 1, L)) < 0.5, rng.integers(0, 2, (N, 8, 1, L)), rng.integers(0, 2, (N, 8, 16, L)))
    T = 4080 * ((np.arange(N)[:, None, None] + np.arange(8)[:, None] + np.arange(RO)) % 2)
    T[:, 2, 1:] = 2040; T[:, 5, 1:] = 1785; T[1:N - 1, 6, 0] = 4079
    T[0, :, 0] = 0; T[N - 1, :, 0] = 4080
    X[..., 0] = 0; X[..., W - 1] = 255; A[..., 0] = 0; A[..., L - 1] = 255; g[..., 0] = 0; g[..., L - 1] = W - 1
    X[0, :, 1, :] = X[0, :, 0, :]; A[0, :, 0, :] = 0; A[0, :, 1, :] = 255
    I[N - 1, :, 15, :] = W - 1
    I[N - 1, :, :15, 0] = 0; I[N - 1, 1::2, 3, 0] = W - 1; I[N - 1, :, 0, W - 1] = W - 1; O[N - 1, :, 0, W - 1] = W - 1
    I[1, :, :, 2] = W - 1
    g[N - 1, :, 1] = 1; O[N - 1, :, :, 1] = 1; I[N - 1, :, 0, 1] = 1
    g[N - 1, :, 2] = W - 2; O[N - 1, :, :, W - 2] = W - 2; I[N - 1, :, 0, W - 2] = W - 2
    return pack(I, X, O, g, A, T)
def setup_inputs_corners(rng):
    I, X, O, g, A, T = parts(rng); h = W // 2; want = (0, 1, CAP - 1, CAP, CAP + 1, L, CAP, 2); c = np.arange(W)
    E = np.zeros((N, W), np.int64); warm = np.zeros((N, 40), np.int64); late = np.full(N, -1)
    for r in range(N):
        for u in range(8):
            n = want[(u + r + 5) % 8]; t0 = (0, 1, 7, 254, 255)[(u + 3 * r) % 5]
            q = rng.permutation(W); hot = q[:40].reshape(2, 20); cold = (q[40:h], q[h:])
            x = rng.integers(100, 256, (16, W)); i = rng.integers(0, 16, W)
            near = np.nonzero(rng.random(W) < 0.5)[0]; x[:, near] = 0; x[i[near], near] = t0; x[(i[near] + 1) % 16, near] = 1
            hs = q[:40]; x[:, hs] = 0; x[i[hs], hs] = t0 * rng.integers(0, 2, 40)
            flip = u % 2 == 1
            X[r, u] = 255 - x if flip else x; A[r, u] = 255 if flip else 0
            e = rng.permutation(W); sa = e[:W // 4]; sb = e[W // 4:h]; dd = e[h:]; sv = np.zeros(W, bool); sv[e[:h]] = True
            cl = rng.integers(0, 2, W); cl[sa] = 0; cl[sb] = 1
            nh = np.where(sv, rng.choice(np.array([NEED, NEED + 1, 16]), W), rng.choice(np.array([0, NEED - 2, NEED - 1]), W))
            rk = (np.arange(16)[:, None] * (2 * rng.integers(0, 8, W) + 1) + rng.integers(0, 16, W)) & 15
            hn = np.where(rk == 0, hot[cl, 0], hot[cl, rng.integers(0, 20, (16, W))])
            cn = np.where(cl == 0, cold[0][rng.integers(0, len(cold[0]), (16, W))], cold[1][rng.integers(0, len(cold[1]), (16, W))])
            I[r, u] = np.where(rk < nh, hn, cn)
            f = np.concatenate([np.array([W - 1, 0]), 1 + rng.permutation(W - 2)]); learn = np.zeros(W, bool); learn[f[:h]] = True
            p1 = rng.integers(0, K, W); p2 = (p1 + 1 + rng.integers(0, K - 1, W)) % K; way = rng.random(W)
            o = dd[rng.integers(0, h, (K, W))]
            one = learn & (way < 0.5); o[p1[one], c[one]] = e[rng.integers(0, h, W)][one]
            own = one & sv & (rng.random(W) < 0.3); o[p1[own], c[own]] = c[own]
            two = learn & (way >= 0.5); o[p1[two], c[two]] = sa[rng.integers(0, W // 4, W)][two]; o[p2[two], c[two]] = sa[rng.integers(0, W // 4, W)][two]
            full = learn & (way >= 0.75); o[:, full] = sb[rng.integers(0, W // 4, (K, W))][:, full]
            apart = ~learn & (way < 0.4); o[p1[apart], c[apart]] = sa[rng.integers(0, W // 4, W)][apart]; o[p2[apart], c[apart]] = sb[rng.integers(0, W // 4, W)][apart]
            O[r, u] = o
            lane = rng.permutation(L); g[r, u, lane[:n]] = f[:n]; g[r, u, lane[n:]] = f[h:h + L - n]
            if u == 7:
                E[r] = e; warm[r] = hs
                if n >= CAP: late[r] = np.sort(lane[:n])[CAP - 1]
            T[r, u, 0] = t0
            if (u + r) % 3 < 2: T[r, u, 1] = 4080 * ((u + r) % 3)
    for r in range(N):
        if late[r] < 0: continue
        z = (r + 1) % N; c0 = int(g[r, 7, late[r]]); s = E[r, :h]; b = s ^ 1
        far = np.max(np.add.reduce(np.abs(X[z, 7][:, I[z, 7][:, b]] - X[z, 7][:, b][:, None, :]), axis=0), axis=0)
        s = s[(far >= 2048) & ~np.isin(s, O[r, 7][:, g[r, 7]]) & ~np.isin(s, warm[r]) & ~np.isin(b, g[z, 7])]
        O[r, 7, :, c0] = E[r, h:][rng.integers(0, h, K)]; O[r, 7, int(rng.integers(0, K)), c0] = rng.choice(s)
    return pack(I, X, O, g, A, T)
def setup_inputs_ties(rng):
    I, X, O, g, A, T = parts(rng); B = 8; c = np.arange(W)
    base = rng.integers(0, 256, (N, 8, 16, B)); sort = np.argsort(rng.random((N, 8, W)), axis=-1) % B; lit = np.argsort(sort, axis=-1, kind="stable")
    rk = (np.arange(16)[:, None] * (2 * rng.integers(0, 8, (N, 8, 1, W)) + 1) + rng.integers(0, 16, (N, 8, 1, W))) & 15
    ty = np.where(rk < rng.integers(NEED - 1, NEED + 1, (N, 8, 1, W)), c % B, (c // B) % B)
    I = take(lit, ty * (W // B) + rng.integers(0, 6, (N, 8, 16, W)))
    X = np.take_along_axis(base, sort[:, :, None, :], 3)
    A = np.take_along_axis(base, rng.integers(0, B, (N, 8, 1, L)), 3); A[..., :16] = base[..., :1]
    O = np.where(rng.random((N, 8, 1, W)) < 0.6, O[:, :, :1] % 64 + 64 * rng.integers(0, W // 64, (N, 8, K, W)), O)
    T[:, :, 0] = np.clip(np.add.reduce(np.abs(base[..., 0] - base[..., 1]), axis=2) + (np.arange(N)[:, None] + np.arange(8)) % 3 - 1, 0, 4080)
    return pack(I, X, O, g, A, T)
def setup_inputs_clash(rng):
    I, X, O, g, A, T = parts(rng)
    q = np.argsort(rng.random((8, W // 2)), axis=-1)[:, :16]; s = np.ascontiguousarray(np.broadcast_to(np.concatenate([2 * q, 2 * q + 1], axis=1), (N, 8, 32)))
    I = np.where(rng.random((N, 8, 16, W)) < 0.8, take(s, rng.integers(0, 32, (N, 8, 16, W))), I)
    O = np.where(rng.random((N, 8, K, W)) < 0.7, take(s, rng.integers(0, 32, (N, 8, K, W))), O)
    g = take(s, rng.integers(0, 32, (N, 8, L))); T = rng.integers(1000, 2600, (N, 8, RO))
    v = rng.integers(0, 21, (N, 3, 16, W)); X[:, 1::3] = np.where(rng.random((N, 3, 1, W)) < 0.5, v, 255 - v)
    v = rng.integers(0, 21, (N, 3, 16, L)); A[:, 1::3] = np.where(rng.random((N, 3, 1, L)) < 0.5, v, 255 - v)
    T[:, 1::3] = rng.integers(3072, 3840, (N, 3, RO))
    return pack(I, X, O, g, A, T)
def check_inputs(d):
    bad = []
    for k, lo, hi in (("icol", 0, W - 1), ("pat", 0, 255), ("alt", 0, W - 1), ("gate", 0, W - 1), ("acc0", 0, 255), ("th", 0, 4080)):
        v = np.asarray(d[k]).astype(np.float64)
        if not (np.min(v) >= lo and np.max(v) <= hi): bad.append("range of " + k)
        elif np.any(v != np.floor(v)): bad.append("whole numbers in " + k)
    return bad
def pick(Xr, n):
    return Xr[np.arange(8).reshape((8,) + (1,) * (n.ndim - 1)), n]
def rewrite(Ir, Xr, c, v, use):
    n = np.take_along_axis(Ir, c[:, None, :], 2)
    far = np.add.reduce(np.abs(pick(Xr, n) - pick(Xr, c)[:, None]), axis=-1); p = np.argmax(far, axis=1)
    for g in range(8):
        j = np.nonzero(use[g])[0]; j = j[np.unique(c[g, j], return_index=True)[1]]
        Ir[g, p[g, j], c[g, j]] = v[g, j]
def reference(icol, pat, alt, gate, acc0, th):
    I = icol.astype(np.int32).reshape(N, 8, 16, W); O = alt.astype(np.int64).reshape(N, 8, K, W); T = th.astype(np.int64)
    X = np.ascontiguousarray(pat.astype(np.float32).astype(np.int32).reshape(N, 8, 16, W).transpose(0, 1, 3, 2))
    A = np.ascontiguousarray(acc0.astype(np.float32).astype(np.int32).reshape(N, 8, 16, L).transpose(0, 1, 3, 2))
    G = np.stack([gentries(a) for a in gate]).astype(np.int64)
    for t in range(RO):
        sent = []
        for r in range(N):
            g = G[r]; o = np.take_along_axis(O[r], g[:, None, :], 2)
            col = np.take_along_axis(I[r], o.reshape(8, 1, K * L), 2).reshape(8, 16, K, L)
            dist = np.add.reduce(np.abs(pick(X[r], col) - A[r][:, None, None, :, :]), axis=-1)
            sv = np.add.reduce((dist <= T[r, :, t].reshape(8, 1, 1, 1)).astype(np.int32), axis=1) >= NEED
            ns = np.add.reduce(sv.astype(np.int32), axis=1); first = np.argmax(sv, axis=1)
            fc = np.take_along_axis(col, first[:, None, None, :], 2)[:, :, 0, :]
            ok = np.ones((8, 16, L), bool)
            for k in range(K):
                ok &= np.any(fc[:, :, None, :] == col[:, None, :, k, :], axis=2) | ~sv[:, None, k, :]
            com = np.take_along_axis(fc, np.argmax(ok, axis=1)[:, None, :], 1)[:, 0].astype(np.int64)
            sole = np.take_along_axis(o, first[:, None, :], 1)[:, 0]
            lrn = (ns == 1) | ((ns >= 2) & np.any(ok, axis=1))
            m = np.where(ns == 1, sole, np.where(lrn, com, o[:, K - 1]))
            rewrite(I[r], X[r], g, m, lrn)
            a = np.zeros((8, CAP), np.int64); b = np.zeros((8, CAP), np.int64); use = np.zeros((8, CAP), bool)
            for u in range(8):
                j = np.nonzero(lrn[u])[0][:CAP]
                a[u, :len(j)] = m[u, j] ^ 1; b[u, :len(j)] = g[u, j] ^ 1; use[u, :len(j)] = True
            sent.append((a, b, use))
            A[r] = np.where(lrn[:, :, None], (A[r] + pick(X[r], m)) >> 1, np.abs(A[r] - pick(X[r], o[:, 0])))
            G[r] = ((m * g >> 4) + 37 * g + int(np.count_nonzero(lrn))) & (W - 1)
        for r in range(N):
            q = (r + 1 + t % (N - 1)) % N; a, b, use = sent[r]
            rewrite(I[q], X[q], a, b, use)
    yc = np.add.reduce(I * np.arange(1, 17, dtype=np.int32).reshape(1, 1, 16, 1), axis=2)
    return {"yc": yc.astype(np.float32), "ya": np.ascontiguousarray(A.transpose(0, 1, 3, 2)).reshape(N, 128, L).astype(np.float32), "yg": G.astype(np.float32)}

@@ -1,0 +1,657 @@
+from concourse.bass import DstId, RemoteDMATransfer
+from concourse.mybir import dt, AluOpType, AxisListType, ActivationFunctionType
+
+W, L, RO, CAP = 4096, 256, 3, 96
+NX = 128
+NF32 = 6
+PARTS = {"c_", "Bc", "Arep", "Rs", "Xcr", "CK", "C16", "OH", "Xar_a", "Xar_v", "d2o"}
+F32, BF, F16, I32, U16 = "float32", "bfloat16", "float16", "int32", "uint16"
+IW = W + 32
+
+SCRATCH = {}
+
+
+def _sb(dtype, **kw):
+    for k, n in kw.items():
+        SCRATCH[k] = ("sbuf", [128, n], dtype)
+
+
+_sb(I32, ic=W, TB=W, gi0=16, gi1=16, thi=4, smi=128)
+_sb(F32, It=IW, Ff=144, FK=128, Gm=128, col=16, rowm=16, thf=4, thc=4, E8=128, Yw=144, smf=272,
+    d10=L, ccf=L, tA=64, OL=48, Nn=48, d2o=32, x2=32,
+    Zt=L, Wp=1536, Tt=192, S0=24, S1=24, S2=24, R0=24, R1=24, R2=24,
+    Bt=L, base=16, dd2=16, dup=16, SD=L, SC=L, tt=L, tu=L, e1=16, e2=16,
+    hA=L, yao=L, ygo=L, yco=L, c3f=CAP)
+_sb(BF, X=W, A=L, nA=L, Arep=16 * NX, Xc=L, Xcr=W, dd=48 * NX, rr=48 * NX, ab=48 * (L - NX), d2=W, a2=W,
+    Bc=2048, Dm=2048, Sa=144, Sb=144, Sm=144, Rs=432, Q=144, Id=128, Id2=128, Idm=128, BO=128, Uu=128, Tm=128,
+    Rk=128, On=128, W16=8, TBK=L, rst=L, RS=L, c75=16, Yh=144, NR0=192, NR1=192, EQ0=512, EQ1=512, e2b=64,
+    LN=32, LB=32, Pq=16, OH=L, dA=L, r23=512, avg=L, Xa=CAP, Xar=16 * CAP)
+_sb(F16, OPT=L, C16=768, cc16=L, A8a=512, A8b=512, FN=768, FS=512, AM=32, dumx=16, b16=16, key=16, g16=16,
+    c316=CAP, Ih=W - 256 * NF32)
+_sb(U16, gu=16, clu=64, CU=1024, CK=768, ccu=L, offu=16, ou=32, mou=16, au=16, c3u=CAP)
+for _k in range(8):
+    SCRATCH["P%d" % _k] = ("psum", [128, 512], F32)
+
+NDMA = 24
+SEMAPHORES = ["sv", "sa", "sp", "sg"] + ["d%d" % k for k in range(NDMA)] + ["arr0", "arr1", "arr2", "snt"]
+
+Alu = AluOpType
+Act = ActivationFunctionType
+
+
+def schedule(g, T, ops):
+    queue = {"v": g.vector, "a": g.scalar, "p": g.tensor, "g": g, "s": g.sync}
+    lastw, readers = {}, {}
+    known = {e: {} for e in queue}
+    waits, clock, needed = [], [], set()
+    for i, o in enumerate(ops):
+        e, asyn = o["e"], o["sem"] is not None
+        deps = set()
+        for r in o["r"]:
+            if r in lastw:
+                deps.add(lastw[r])
+        for r in o["w"]:
+            prev = list(readers.get(r, [])) + ([lastw[r]] if r in lastw else [])
+            for j in prev:
+                same = ops[j]["e"] == e and ops[j]["sem"] is None and not asyn
+                part = j == lastw.get(r) and (r in PARTS or r.startswith("ab"))
+                if j != i and (not same or (e != "p" and not r[1:].isdigit() and not part)):
+                    deps.add(j)
+        w = []
+        if o["f"] is not None:
+            for j in sorted(deps, reverse=True):
+                chan = ops[j]["sem"] or ops[j]["e"]
+                if known[e].get(chan, -1) >= j:
+                    continue
+                w.append(j)
+                needed.add(j)
+                for c, v in clock[j].items():
+                    if known[e].get(c, -1) < v:
+                        known[e][c] = v
+        waits.append(w)
+        ck = dict(known[e]) if o["f"] is not None else {}
+        ck[o["sem"] or e] = i
+        clock.append(ck)
+        for r in o["r"]:
+            readers.setdefault(r, []).append(i)
+        for r in o["w"]:
+            lastw[r] = i
+            readers[r] = []
+    count, val = {}, {}
+    for i, o in enumerate(ops):
+        q = queue[o["e"]]
+        for j in waits[i]:
+            q.wait_ge(T.sem[val[j][0]], val[j][1])
+        if o["sem"] is not None:
+            count[o["sem"]] = count.get(o["sem"], 0) + o["n"]
+            val[i] = (o["sem"], count[o["sem"]])
+            if o["f"] is not None:
+                ins = o["f"]()
+                if o["inc"]:
+                    ins.then_inc(T.sem[o["sem"]], o["n"])
+        else:
+            ins = o["f"]()
+            if i in needed:
+                s = "s" + o["e"]
+                count[s] = count.get(s, 0) + 1
+                val[i] = (s, count[s])
+                ins.then_inc(T.sem[s], 1)
+
+
+def rank_program(g, core, T, topo):
+    if T.rank_of(core) is not None:
+        program(g, core, T, topo)
+
+
+def program(g, core, T0, topo):
+    def sf(j):
+        return [T0.smf[:, 16 * j:16 * j + 16]]
+
+    def si(j, n=16):
+        return [T0.smi[:, 16 * j:16 * j + n]]
+
+    class T:
+        icol, pat, alt, gate, acc0, th, yc, ya, yg = T0.icol, T0.pat, T0.alt, T0.gate, T0.acc0, T0.th, T0.yc, T0.ya, T0.yg
+        sem, cores = T0.sem, T0.cores
+        kc, ri, pi, mi, t1, mc, sh, gs = si(0, 1), si(1, 1), si(2, 1), si(3), si(4), si(5), si(6), si(7)
+        (Dl, la, lb, one, two, none1, mdef, pre, hh, ww, t2, yy, offf, cm, ddm, c37, c37e) = [sf(j) for j in range(17)]
+        (ic, TB, gi0, thi, It, Ff, FK, Gm, col, rowm, thf, thc, E8, Yw, d10, ccf, tA, OL, Nn, d2o, x2, Zt, Wp, Tt, Bt, base,
+         dd2, dup, SD, SC, tt, tu, e1, e2, hA, yao, ygo, yco, c3f) = [T0[k] for k in (
+             "ic TB gi0 thi It Ff FK Gm col rowm thf thc E8 Yw d10 ccf tA OL Nn d2o x2 Zt Wp Tt Bt base "
+             "dd2 dup SD SC tt tu e1 e2 hA yao ygo yco c3f").split()]
+        (X, A, nA, Arep, Xc, Xcr, dd, rr, ab, d2, a2, Bc, Dm, Sa, Sb, Sm, Rs, Q, Id, Id2, Idm, BO, Uu, Tm, Rk, On, W16,
+         TBK, rst, RS, c75, Yh, e2b, LN, LB, Pq, OH, dA, r23, avg, Xa, Xar) = [T0[k] for k in (
+             "X A nA Arep Xc Xcr dd rr ab d2 a2 Bc Dm Sa Sb Sm Rs Q Id Id2 Idm BO Uu Tm Rk On W16 "
+             "TBK rst RS c75 Yh e2b LN LB Pq OH dA r23 avg Xa Xar").split()]
+        (OPT, C16, cc16, A8a, A8b, FN, FS, AM, dumx, b16, key, g16, c316, Ih, gu, clu, CU, CK, ccu, offu, ou, mou, au,
+         c3u) = [T0[k] for k in ("OPT C16 cc16 A8a A8b FN FS AM dumx b16 key g16 c316 Ih gu clu CU CK ccu offu ou mou au "
+                                 "c3u").split()]
+
+    rank = T0.rank_of(core)
+    N = len(T.cores)
+    ops = []
+    nd = [0]
+    V, S, PE = g.vector, g.scalar, g.tensor
+
+    def names(x):
+        return x.split() if isinstance(x, str) else list(x)
+
+    def un(x):
+        return x[0] if isinstance(x, list) else x
+
+    def op(e, f, r, w, sem=None, n=0, inc=False):
+        r, w = names(r), names(w)
+        banks = [x for x in r if x[0] == "P" and x[1:].isdigit()]
+        ops.append({"e": e, "f": f, "r": [x for x in r if x not in banks], "w": w + banks, "sem": sem, "n": n, "inc": inc})
+
+    def dma(e, out, in_, r, w):
+        q = {"s": g.sync, "a": g.scalar}[e]
+        op(e, lambda: q.dma_start(out, in_), r, w, sem="d%d" % nd[0], n=16, inc=True)
+        nd[0] += 1
+
+    def ts(out, in0, s1, s2, o0, o1, r, w):
+        if o1 is None:
+            op("v", lambda: V.tensor_scalar(un(out), un(in0), s1, None, o0), r, w)
+        else:
+            op("v", lambda: V.tensor_scalar(un(out), un(in0), s1, s2, o0, o1), r, w)
+
+    def tt(out, a, b, o, r, w):
+        op("v", lambda: V.tensor_tensor(un(out), un(a), un(b), o), r, w)
+
+    def cp(out, a, r, w):
+        op("v", lambda: V.tensor_copy(un(out), un(a)), r, w)
+
+    def ms(out, c, w):
+        op("v", lambda: V.memset(out, c), "", w)
+
+    def mm(out, l, rh, st, sp, r, w):
+        op("p", lambda: PE.matmul(out, l, rh, st, sp), r, w)
+
+    def act(out, in_, fn, r, w, bias=None, scale=None):
+        kw = {}
+        if bias is not None:
+            kw["bias"] = bias
+        if scale is not None:
+            kw["scale"] = scale
+        op("a", lambda: S.activation(out, in_, fn, **kw), r, w)
+
+    def iota(out, pat, base, cm, w, small=True):
+        if small:
+            op("g", lambda: g.iota(out, pat, base, cm, allow_small_or_imprecise_dtypes=True), "", w)
+        else:
+            op("g", lambda: g.iota(un(out), pat, base, cm), "", w)
+
+    P = [T0["P%d" % k] for k in range(8)]
+    Xw, Iw = T.X[:, 0:W], T.It[:, 0:IW]
+    col = T.col
+    RF, G16, G15, K12, RLT3, RP1, R256, PAR, M8, A8C, R2A, R2B, YB, K16, BM, BMN = [col[:, j:j + 1] for j in range(16)]
+    MAGIC = 12582912.0
+    MAG16 = 201326592.0
+
+    ms(T.TB[:], 0, "TB0")
+    dma("s", T.gi0[:], T.gate[:], "", "gi0")
+    for j in range(4):
+        dma("s", T.ic[:, 1024 * j:1024 * j + 1024], T.icol[:, 1024 * j:1024 * j + 1024], "", "ic%d" % j)
+    dma("a", T.A[:], T.acc0[:], "", "A")
+    dma("a", T.thi[0:8, 0:3], T.th[:], "", "thi")
+    for u in range(8):
+        dma("s", T.TB[16 * u:16 * u + 3, :], T.alt[3 * u:3 * u + 3, :], "TB0", "TB_%d" % u)
+    dma("s", T.X[:], T.pat[:], "", "X")
+    TBall = "TB0 " + " ".join("TB_%d" % u for u in range(8))
+
+    iota(T.kc[:], [[0, 1]], 0, 1, "kc", small=False)
+    iota(T.Ff[:], [[1, 144]], 0, 0, "Ff")
+    iota(T.Gm[:], [[16, 8], [0, 16]], 0, 0, "Gm")
+    iota(T.FK[:], [[1, 128]], 0, -1, "FK")
+    iota(T.TBK[:], [[0, 16], [-1, 16]], 15, 0, "TBK")
+    ts(T.ri[:], T.kc[:], 15, None, Alu.bitwise_and, None, "kc", "ri")
+    ts(T.pi[:], T.kc[:], 16, None, Alu.bitwise_and, None, "kc", "pi")
+    cp(RF, T.ri[:], "ri", "RF")
+    tt(G16, T.kc[:], T.ri[:], Alu.subtract, "kc ri", "G16")
+    ts(K12, T.kc[:], 12.0, None, Alu.add, None, "kc", "c_")
+    ts(K16, T.kc[:], 16.0, None, Alu.mult, None, "kc", "c_")
+    ts(RLT3, T.ri[:], 2.5, None, Alu.is_lt, None, "ri", "c_")
+    ts(RP1, T.ri[:], 1.0, None, Alu.add, None, "ri", "c_")
+    ts(R256, T.ri[:], 256.0, None, Alu.add, None, "ri", "c_")
+    ts(PAR, T.pi[:], 7.5, None, Alu.add, None, "pi", "c_")
+    ts(M8, T.ri[:], 8.0, None, Alu.is_equal, None, "ri", "M8")
+    ts(R2A, T.ri[:], 2.0, 2048.0, Alu.mult, Alu.add, "ri", "c_")
+    ts(R2B, T.ri[:], 2.0, 6144.0, Alu.mult, Alu.add, "ri", "c_")
+    ts(YB, T.ri[:], NF32 - 0.5, 2048.0 * 136, Alu.is_gt, Alu.mult, "ri", "c_")
+    ms(BM, MAGIC, "c_")
+    ms(BMN, -MAGIC, "c_")
+    ts(G15, G16, 15.0, None, Alu.add, None, "G16", "c_")
+    ts(A8C, M8, 12288.0, -4096.0, Alu.mult, Alu.add, "M8", "c_")
+    CC = "c_ RF G16 M8"
+    ts(T.rowm[:], T.Ff[:, 0:16], RF, None, Alu.is_equal, None, "Ff " + CC, "rowm")
+    ts(T.BO[:], T.Gm[:], G16, None, Alu.is_equal, None, "Gm " + CC, "BO")
+    ts(T.Q[:], T.Ff[:], K12, RLT3, Alu.is_equal, Alu.mult, "Ff " + CC, "Q")
+    cp(T.gu[:], T.gi0[:], "gi0", "gu")
+    for s in range(16):
+        act(T.Bc[:, 128 * s:128 * s + 128], T.BO[:], Act.Identity, "BO rowm", "Bc", scale=T.rowm[:, s:s + 1])
+    op("g", lambda: g.affine_select(T.Dm[:], T.Bc[:], [[0, 16], [-16, 8], [-1, 16]], Alu.not_equal, -1.0, 0, 1), "Bc", "Dm")
+    op("g", lambda: g.affine_select(T.Dm[:], T.Dm[:], [[-1, 16], [0, 8], [1, 16]], Alu.is_gt, 0.0, 0, 0), "Dm", "Dm")
+    act(T.nA[:, NX:L], T.A[:, NX:L], Act.Identity, "A", "nA", scale=-1.0)
+
+    def arep():
+        for p in range(16):
+            act(T.Arep[:, p::16], T.A[:, 0:NX], Act.Copy, "A", "Arep")
+    arep()
+    cp(T.It[:, 0:1024], T.ic[:, 0:1024], "ic0", "It")
+    ts(T.Sa[:], T.Ff[:], G15, None, Alu.is_equal, None, "Ff " + CC, "Sa")
+    ts(T.Sb[:], T.Ff[:], G15, 2.0, Alu.is_equal, Alu.mult, "Ff " + CC, "Sb")
+    ts(T.Sm[:], T.Ff[:], G15, -1.0, Alu.is_equal, Alu.mult, "Ff " + CC, "Sm")
+    for k in range(3):
+        ts(T.Rs[:, 144 * k:144 * k + 144], T.Ff[:], G15, T.rowm[:, k:k + 1], Alu.is_equal, Alu.mult, "Ff rowm " + CC, "Rs")
+    ts(T.Id[:], T.FK[:], 0.0, None, Alu.is_equal, None, "FK", "Id")
+    ms(T.It[:, W:IW], 0.0, "It")
+    cp(T.It[:, 1024:2048], T.ic[:, 1024:2048], "ic1", "It")
+    ts(T.Id2[:], T.FK[:], 0.0, 2.0, Alu.is_equal, Alu.mult, "FK", "Id2")
+    ts(T.Idm[:], T.FK[:], 0.0, -1.0, Alu.is_equal, Alu.mult, "FK", "Idm")
+    ts(T.Uu[:], T.FK[:], 0.0, None, Alu.is_gt, None, "FK", "Uu")
+    ts(T.E8[0:8, :], T.Gm[0:8, :], col[0:8, 13:14], None, Alu.is_equal, None, "Gm " + CC, "E8")
+    cp(T.thf[0:8, 0:3], T.thi[0:8, 0:3], "thi", "thf")
+    tt(T.Uu[:], T.Uu[:], T.BO[:], Alu.mult, "Uu BO", "Uu")
+    mm(P[0][:, 0:3], T.E8[0:8, :], T.thf[0:8, 0:3], True, True, "E8 thf", "P0")
+    ts(T.W16[:], T.Gm[:, 0::16], G16, 16.0, Alu.is_equal, Alu.mult, "Gm " + CC, "W16")
+    tt(T.Tm[:], T.Id[:], T.Uu[:], Alu.subtract, "Id Uu", "Tm")
+    tt(T.Rk[:], T.Uu[:], T.BO[:], Alu.subtract, "Uu BO", "Rk")
+    cp(T.It[:, 2048:3072], T.ic[:, 2048:3072], "ic2", "It")
+    ts(T.Tm[:], T.Tm[:], 8192.0, None, Alu.mult, None, "Tm", "Tm")
+    cp(T.thc[:, 0:3], P[0][:, 0:3], "P0", "thc")
+    ms(T.On[:], 1.0, "On")
+    ms(T.c75[:], -7.5, "c75")
+    ts(T.rst[:], T.TBK[:], 15.0, None, Alu.not_equal, None, "TBK", "rst")
+    ts(T.RS[:], T.TBK[:], RF, None, Alu.is_ge, None, "TBK " + CC, "RS")
+    ts(T.Dl[:], T.Ff[:, 0:16], 16.0, R256, Alu.mult, Alu.add, "Ff " + CC, "Dl")
+    for t in range(RO):
+        ms(T0["S%d" % t][:], 0.0, "S%d" % t)
+    cp(T.It[:, 3072:4096], T.ic[:, 3072:4096], "ic3", "It")
+
+    def rep(out_bank, c0, n, rhs, r):
+        for s in range(16):
+            mm(P[out_bank][:, c0 + s:c0 + n:16], T.Bc[:, 128 * s:128 * s + 128], rhs, True, True, "Bc " + r, "P%d" % out_bank)
+
+    def options_first():
+        ts(T.OPT[:], T.TB[:, 0:W].indirect(T.gu[:]), -2048.0, None, Alu.add, None, TBall + " gu", "OPT")
+        for u in range(4):
+            mm(P[5][:, 0:64], T.Q[:, 12 - 4 * u:140 - 4 * u], T.OPT[:, u::4], u == 0, u == 3, "Q OPT", "P5")
+        ts(T.clu[:], P[5][:, 0:64], 2048.0, None, Alu.add, None, "P5", "clu")
+
+    def options_rest(gi, gn):
+        for k in range(3):
+            for s in range(16):
+                mm(P[5][:, 64 + 16 * k:80 + 16 * k], T.Rs[:, 144 * k + 15 - s:144 * k + 143 - s], T.OPT[:, s::16],
+                   s == 0, s == 15, "Rs OPT", "P5")
+        ts(T.t1[:], gi[:], 1, None, Alu.bitwise_and, None, gn, "t1")
+        ts(T.cm[:], gi[:], -2048.0, None, Alu.add, None, gn, "cm")
+        ts(T.t2[:], T.t1[:], -2.0, 1.0, Alu.mult, Alu.add, "t1", "t2")
+        ts(T.c37[:], gi[:], 37.0, None, Alu.mult, None, gn, "c37")
+        tt(T.b16[:], T.t2[:], T.cm[:], Alu.add, "t2 cm", "b16")
+        ts(T.ddm[:], T.cm[:], -1.0, R2A, Alu.mult, Alu.add, "cm " + CC, "ddm")
+        cp(T.OL[:], P[5][:, 64:112], "P5", "OL")
+        rep(6, 0, L, T.b16[:], "b16")
+        tt(T.d2o[:, 0:16], T.OL[:, 0:16], T.OL[:, 32:48], Alu.subtract, "OL", "d2o")
+        tt(T.d2o[:, 16:32], T.OL[:, 16:32], T.OL[:, 32:48], Alu.subtract, "OL", "d2o")
+        ms(T.Wp[:, 0:192], -4096.0, "Wp")
+        ts(T.Bt[:], P[6][:, 0:L], M8, A8C, Alu.mult, Alu.add, "P6 " + CC, "Bt")
+
+    def gate_patterns():
+        act(T.Xc[:], Xw.indirect(T.gu[:]), Act.Copy, "X gu", "Xc")
+        for p in range(16):
+            op("g", lambda p=p: g.affine_select(T.Xcr[:, p::16], T.Xc[:], [[0, L]], Alu.is_ge, 0.0, 0, 0), "Xc", "Xcr")
+
+    def segs(c):
+        lo, hi = 64 * c, 64 * c + 64
+        out = []
+        if lo < NX:
+            out.append(("v", lo, min(hi, NX) - lo, 0))
+        if hi > NX:
+            a = max(lo, NX)
+            if c == 3 and hi - a == 64:
+                out += [("a", a, 32, 0), ("a", a + 32, 32, 96)]
+            else:
+                out.append(("a", a, hi - a, 3 * (a - lo)))
+        return out
+
+    def t1v(c, k):
+        e, lo, n, c0 = segs(c)[0]
+        o = 48 * lo + 16 * n * k
+        nm = "dd%d%d" % (c, k)
+        tt(T.dd[:, o:o + 16 * n], Xw.indirect(T.CK[:, 256 * k + lo:256 * k + lo + n]), T.Arep[:, 16 * lo:16 * (lo + n)],
+           Alu.subtract, "X CK Arep", nm)
+        ts(T.rr[:, o:o + 16 * n], T.dd[:, o:o + 16 * n], 0.0, None, Alu.max, None, nm, "r" + nm)
+        b = c % 2
+        for p in range(16):
+            mm(P[b][:, n * k:n * k + n], T.Sm[:, 15 - p:143 - p], T.dd[:, o + p:o + 16 * n:16], p == 0, False, "Sm " + nm, "P%d" % b)
+        for p in range(16):
+            mm(P[b][:, n * k:n * k + n], T.Sb[:, 15 - p:143 - p], T.rr[:, o + p:o + 16 * n:16], False, p == 15, "Sb r" + nm, "P%d" % b)
+
+    def t1a(lo, n):
+        for l in range(lo, lo + n):
+            o = 48 * (l - NX)
+            act(T.ab[:, o:o + 48], Xw.indirect(T.CU[:, 4 * l:4 * l + 3]), Act.Abs, "X CUa nA", "ab%d" % lo, bias=T.nA[:, l:l + 1])
+
+    def suma(c, lo, n, c0):
+        o = 48 * (lo - NX)
+        b = c % 2
+        for p in range(16):
+            mm(P[b][:, c0:c0 + 3 * n], T.Sa[:, 15 - p:143 - p], T.ab[:, o + p:o + 48 * n:16], p == 0, p == 15, "Sa ab%d" % lo, "P%d" % b)
+
+    def near(c, t):
+        b = c % 2
+        NR = T0["NR%d" % b]
+        ts(NR[:], P[b][:, 0:192], T.thc[:, t:t + 1], None, Alu.is_le, None, "thc P%d" % b, "NR%d" % b)
+        for e, lo, n, c0 in segs(c):
+            for k in range(3):
+                rhs = NR[:, c0 + n * k:c0 + n * k + n] if e == "v" else NR[:, c0 + k:c0 + 3 * n:3]
+                o = 256 + 64 * k + lo - 64 * c
+                mm(P[b][:, o:o + n], T.BO[:], rhs, True, True, "BO NR%d" % b, "P%d" % b)
+
+    def rot(c, j):
+        b = 2 + j % 2
+        for i in range(4):
+            s = 4 * j + i
+            for h in range(2):
+                mm(P[b][:, 128 * i + 64 * h:128 * i + 64 * h + 64], T.Bc[:, 128 * s:128 * s + 128],
+                   T.C16[:, 256 * (h + 1) + 64 * c:256 * (h + 1) + 64 * c + 64], True, True, "Bc C16", "P%d" % b)
+
+    def first_col(c):
+        b = c % 2
+        A8, an = (T.A8a, "A8a") if b == 0 else (T.A8b, "A8b")
+        lo = 64 * c
+        for k in range(3):
+            ts(T.FN[:, 256 * k + lo:256 * k + lo + 64], P[b][:, 256 + 64 * k:320 + 64 * k], 7.5, None, Alu.is_lt, None,
+               "P%d" % b, "FN%d%d" % (c, k))
+        tt(T.tA[:], T.FN[:, lo:lo + 64], T.d10[:, lo:lo + 64], Alu.mult, "d10 FN%d0" % c, "tA")
+        tt(A8[:, 0:64], T.tA[:], T.C16[:, lo:lo + 64], Alu.add, "tA C16", an)
+        for n in (64, 128, 256):
+            cp(A8[:, n:2 * n], A8[:, 0:n], an, an)
+
+    def member(c):
+        b = c % 2
+        A8, an = (T.A8a, "A8a") if b == 0 else (T.A8b, "A8b")
+        for j in range(4):
+            EQ = T0["EQ%d" % (j % 2)]
+            tt(EQ[:], A8[:], P[2 + j % 2][:], Alu.is_equal, an + " P%d" % (2 + j % 2), "EQ%d" % (j % 2))
+            if j < 2:
+                rot(c, j + 2)
+            elif c < 3:
+                rot(c + 1, j - 2)
+            for i in range(4):
+                mm(P[4][:, 0:128], T.Id[:], EQ[:, 128 * i:128 * i + 128], j == 0 and i == 0, j == 3 and i == 3,
+                   "Id EQ%d" % (j % 2), "P4")
+            if j == 0:
+                for h in range(2):
+                    o = 256 * (h + 1) + 64 * c
+                    mm(P[4][:, 64 * h:64 * h + 64], T.Id[:], T.FN[:, o:o + 64], False, False, "Id FN%d%d" % (c, h + 1), "P4")
+
+    def okrows(c):
+        b = c % 2
+        A8, an = (T.A8a, "A8a") if b == 0 else (T.A8b, "A8b")
+        o = 256 + 64 * c
+        ts(T.e2b[:], P[4][:, 64:128], 1.0, None, Alu.min, None, "P4", "e2b")
+        tt(T.FS[:, o:o + 64], T.e2b[:], P[4][:, 0:64], Alu.min, "e2b P4", "FSo%d" % c)
+        mm(P[4][:, 256:320], T.Id[:], A8[:, 0:64], True, False, "Id " + an, "P4")
+        mm(P[4][:, 256:320], T.Tm[:], T.FS[:, o:o + 64], False, True, "Tm FSo%d" % c, "P4")
+
+    def selrow(c):
+        ts(T.FS[:, 64 * c:64 * c + 64], P[4][:, 256:320], -8192.0, -2048.0, Alu.add, Alu.max, "P4", "FSs%d" % c)
+
+    def s2gather(u):
+        o = 1024 * u
+        tt(T.d2[:, o:o + 1024], Xw.indirect(T.ccu[:, 64 * u:64 * u + 64]), T.Xcr[:, o:o + 1024], Alu.subtract, "X ccu Xcr", "d2%d" % u)
+
+    def s2abs(u):
+        o = 1024 * u
+        act(T.a2[:, o:o + 1024], T.d2[:, o:o + 1024], Act.Abs, "d2%d" % u, "a2%d" % u)
+
+    def farthest(n, halves, r):
+        w = 128 * halves
+        mm(P[7][0:n, 0:w], T.Id[:, 0:n], T.TBK[:, 0:w], True, False, "Id TBK", "P7")
+        for h in range(halves):
+            for p in range(16):
+                mm(P[7][0:n, 128 * h + p:128 * h + 128:16], T.a2[:, 2048 * h + p:2048 * h + 16 * n:16], T.W16[:], False,
+                   h == halves - 1 and p == 15, "W16 " + r[h], "P7")
+
+    def onehot(n, halves):
+        w = 128 * halves
+        op("v", lambda: V.tensor_tensor_scan(T.SC[0:n, 0:w], T.rst[0:n, 0:w], P[7][0:n, 0:w], 0.0, Alu.mult, Alu.max), "rst P7", "SC")
+        for u in range(8 * halves):
+            ts(T.OH[0:n, 16 * u:16 * u + 16], P[7][0:n, 16 * u:16 * u + 16], T.SC[0:n, 16 * u + 15:16 * u + 16], None,
+               Alu.is_equal, None, "SC P7", "OH")
+        for h in range(halves):
+            mm(P[7][:, 256 + 128 * h:256 + 128 * h + n], T.OH[0:n, 128 * h:128 * h + 128], T.Id[0:n, 0:n], True, True, "OH Id", "P7")
+
+    def dedupe_a(nq):
+        ts(T.key[:, 0:nq], T.base[:, 0:nq], 1.0 / 64, None, Alu.mult, None, "base", "key")
+        for s in range(16):
+            mm(P[4][:, 15 - s:16 * nq:16], T.Dm[:, 128 * s:128 * s + 128], T.key[:, 0:nq], True, True, "Dm key", "P4")
+        ts(T.dd2[:, 0:nq], T.base[:, 0:nq], -1.0, R2A, Alu.mult, Alu.add, "base " + CC, "dd2")
+
+    def dedupe_b(nq):
+        w = 16 * nq
+        op("v", lambda: V.tensor_tensor_scan(T.SD[:, 0:w], P[4][:, 0:w], T.RS[:, 0:w], 1.0, Alu.mult, Alu.add), "RS P4", "SD")
+        ts(T.dup[:, 0:nq], T.SD[:, 15:w:16], 0.0, None, Alu.is_equal, None, "SD", "dup")
+        tt(T.e1[:, 0:nq], T.dup[:, 0:nq], T.dd2[:, 0:nq], Alu.mult, "dup dd2", "e1")
+        tt(T.e2[:, 0:nq], T.e1[:, 0:nq], T.base[:, 0:nq], Alu.add, "e1 base", "e2")
+        ts(T.ou[:, 0:2 * nq:2], T.e2[:, 0:nq], 2048.0, None, Alu.add, None, "e2", "ou")
+
+    def write_cols(nq, cf, cn):
+        n = 16 * nq
+        tt(T.tu[:, 0:n], T.tt[:, 0:n], P[7][:, 256:256 + n], Alu.mult, "tt P7", "tu")
+        for q in reversed(range(nq)):
+            tt(Iw.indirect(T.ou[:, 2 * q:2 * q + 1]), cf[:, 16 * q:16 * q + 16], T.tu[:, 16 * q:16 * q + 16], Alu.add,
+               "ou tu " + cn, "It")
+
+    options_first()
+    gate_patterns()
+    for t in range(RO):
+        gi, gn = T0["gi%d" % (t % 2)], "gi%d" % (t % 2)
+        gj, gm = T0["gi%d" % ((t + 1) % 2)], "gi%d" % ((t + 1) % 2)
+        last = t == RO - 1
+        St, sn = T0["S%d" % t], "S%d" % t
+        Rt, rn = T0["R%d" % t], "R%d" % t
+        cp(T.CU[:, 4 * NX:1024], Iw.indirect(T.clu[:, NX // 4:64]), "It clu", "CUa")
+        asegs = [(c, s) for c in range(4) for s in segs(c) if s[0] == "a"]
+        for c, s in asegs:
+            t1a(s[1], s[2])
+        cp(T.CU[:, 0:4 * NX], Iw.indirect(T.clu[:, 0:NX // 4]), "It clu", "CUv")
+        for k in range(3):
+            cp(T.CK[:, 256 * k:256 * k + NX], T.CU[:, k:4 * NX:4], "CUv", "CK")
+        for k in range(3):
+            t1v(0, k)
+        options_rest(gi, gn)
+        for k in range(3):
+            ts(T.C16[:, 256 * k:256 * k + 256], T.CU[:, k::4], -2048.0, None, Alu.add, None, "CUa CUv", "C16")
+        tt(T.d10[:], T.C16[:, 256:512], T.C16[:, 0:256], Alu.subtract, "C16", "d10")
+        t1v(1, 0)
+        near(0, t)
+        rot(0, 0)
+        rot(0, 1)
+        t1v(1, 1)
+        t1v(1, 2)
+        for c, s in asegs:
+            if c == 1:
+                suma(c, s[1], s[2], s[3])
+        first_col(0)
+        cp(T.ccu[:], Iw.indirect(T.gu[:]), "It gu", "ccu")
+        for c, s in asegs:
+            if c == 2:
+                suma(c, s[1], s[2], s[3])
+        member(0)
+        near(1, t)
+        okrows(0)
+        s2gather(0)
+        first_col(1)
+        selrow(0)
+        near(2, t)
+        member(1)
+        first_col(2)
+        okrows(1)
+        s2gather(1)
+        selrow(1)
+        a3 = [s for c, s in asegs if c == 3]
+        for s in a3[:-1]:
+            suma(3, s[1], s[2], s[3])
+        member(2)
+        okrows(2)
+        suma(3, a3[-1][1], a3[-1][2], a3[-1][3])
+        s2gather(2)
+        selrow(2)
+        near(3, t)
+        ts(T.cc16[:], T.ccu[:], -2048.0, None, Alu.add, None, "ccu", "cc16")
+        first_col(3)
+        for u in range(3):
+            s2abs(u)
+        FNall = " ".join("FN%d%d" % (c, k) for c in range(4) for k in range(3))
+        member(3)
+        for s in range(16):
+            mm(P[5][:, 160:208], T.Sa[:, 15 - s:143 - s], T.FN[:, s::16], s == 0, s == 15, "Sa " + FNall, "P5")
+        okrows(3)
+        ts(T.Nn[:], P[5][:, 160:208], -1.0 / 16, 1.0, Alu.mult, Alu.add, "P5", "Nn")
+        selrow(3)
+        FSall = " ".join("FS%s%d" % (x, c) for c in range(4) for x in "so")
+        for s in range(16):
+            mm(P[5][:, 128:160], T.Sa[:, 15 - s:143 - s], T.FS[:, s::16], s == 0, s == 15, "Sa " + FSall, "P5")
+        tt(T.la[:], T.Nn[:, 0:16], T.Nn[:, 16:32], Alu.add, "Nn", "la")
+        tt(T.x2[:], T.Nn[:, 0:32], T.d2o[:], Alu.mult, "Nn d2o", "x2")
+        tt(T.la[:], T.la[:], T.Nn[:, 32:48], Alu.add, "la Nn", "la")
+        tt(T.lb[:], T.x2[:, 0:16], T.x2[:, 16:32], Alu.add, "x2", "lb")
+        ts(T.one[:], T.la[:], 1.0, None, Alu.is_equal, None, "la", "one")
+        ts(T.two[:], T.la[:], 1.5, None, Alu.is_gt, None, "la", "two")
+        ts(T.none1[:], T.la[:], 1.0, None, Alu.not_equal, None, "la", "none1")
+        tt(T.lb[:], T.lb[:], T.one[:], Alu.mult, "lb one", "lb")
+        tt(T.hh[:], T.two[:], P[5][:, 144:160], Alu.min, "two P5", "hh")
+        tt(T.mdef[:], T.lb[:], T.OL[:, 32:48], Alu.add, "lb OL", "mdef")
+        tt(T.LN[:, 16:32], T.hh[:], T.one[:], Alu.add, "hh one", "lrn")
+        tt(T.LN[:, 0:16], T.none1[:], T.hh[:], Alu.subtract, "none1 hh", "nl")
+        tt(T.pre[:], P[5][:, 128:144], T.mdef[:], Alu.subtract, "mdef P5", "pre")
+        op("v", lambda: V.tensor_tensor_scan(T.Pq[:], T.On[:, 0:16], T.LN[:, 16:32], 0.0, Alu.mult, Alu.add), "On lrn", "Pq")
+        tt(T.dumx[:], T.LN[:, 0:16], T.Dl[:], Alu.mult, "nl Dl", "dumx")
+        ts(T.pre[:], T.pre[:], 30720.0, None, Alu.add, None, "pre", "pre")
+        mm(P[5][:, 224:240], T.Id[:], T.c75[:], True, False, "Id c75", "P5")
+        mm(P[5][:, 224:240], T.Rk[:], T.LN[:, 16:32], False, False, "Rk lrn", "P5")
+        mm(P[5][:, 224:240], T.BO[:], T.Pq[:], False, False, "BO Pq", "P5")
+        mm(P[5][:, 224:240], T.Id[:], T.dumx[:], False, True, "Id dumx", "P5")
+        mm(P[5][:, 240:241], T.On[:], T.Pq[:, 15:16], True, True, "On Pq", "P5")
+        act(T.LB[:], T.LN[:], Act.Identity, "lrn nl", "LB", scale=-1024.0)
+        tt(T.ww[:], T.pre[:], T.hh[:], Alu.mult, "pre hh", "ww")
+        tt(T.AM[:, 16:32], T.ww[:], T.mdef[:], Alu.add, "ww mdef", "m16")
+        ts(T.mi[:], T.AM[:, 16:32], 2048.0, None, Alu.add, None, "m16", "mi")
+        ts(T.yy[:], P[5][:, 224:240], MAG16, -MAG16, Alu.add, Alu.add, "P5", "yy")
+        ts(T.t1[:], T.mi[:], 1, None, Alu.bitwise_and, None, "mi", "t1")
+        tt(T.offf[:], T.yy[:], P[5][:, 224:240], Alu.add, "yy P5", "offf")
+        ts(T.t2[:], T.t1[:], -2.0, 1.0, Alu.mult, Alu.add, "t1", "t2")
+        ts(T.offu[:], T.offf[:], PAR, None, Alu.add, None, "offf " + CC, "offu")
+        tt(T.AM[:, 0:16], T.t2[:], T.AM[:, 16:32], Alu.add, "t2 m16", "a16")
+        rep(6, 0, 512, T.AM[:], "a16 m16")
+        ts(T.c37e[:], T.c37[:], P[5][:, 240:241], None, Alu.add, None, "c37 P5", "c37e")
+        tt(T.mc[:], T.mi[:], gi[:], Alu.mult, "mi " + gn, "mc")
+        tt(T.e1[:], T.LN[:, 0:16], T.ddm[:], Alu.mult, "nl ddm", "e1")
+        ts(T.sh[:], T.mc[:], 4, None, Alu.arith_shift_right, None, "mc", "sh")
+        tt(T.base[:], T.e1[:], T.cm[:], Alu.add, "e1 cm", "base")
+        tt(T.Zt[:], T.Bt[:], P[6][:, 0:L], Alu.max, "Bt P6", "Zt")
+        cp(T.Wp[:, 0:1536].indirect(T.offu[:]), T.Zt[:], "offu Zt", "Wp")
+        op("v", lambda: V.transpose(T.Tt[:], T.Wp[:, 0:192]), "Wp", "Tt")
+        tt(St[:, 0:22], T.Tt[:, 0:176:8], T.Tt[:, 16:192:8], Alu.max, "Tt", sn)
+        dst = T.cores[(rank + 1 + t % (N - 1)) % N]
+        src = T.cores[(rank - 1 - t % (N - 1)) % N]
+        rid, pid = topo.addr(dst)[0], topo.addr(dst)[1]
+        eng = topo.engines(core, dst)[::2]
+        mask = sum(1 << x for x in eng)
+        op("g", lambda St=St, Rt=Rt, t=t, pid=pid, rid=rid, mask=mask:
+           g.remote_dma(Rt[:], St[:], T.sem["arr%d" % t], T.sem.snt, pid, rid, mask), sn, "sent", sem="snt", n=len(eng))
+        op("g", None, "", rn, sem="arr%d" % t, n=len(topo.engines(src, core)[::2]))
+        s2gather(3)
+        s2abs(3)
+        farthest(128, 2, ["a20 a21", "a22 a23"])
+        dedupe_a(16)
+        tt(T.gs[:], T.sh[:], T.c37e[:], Alu.add, "sh c37e", "gs")
+        tt(T.e2[:], T.AM[:, 16:32], T.OL[:, 0:16], Alu.subtract, "m16 OL", "e2")
+        ts(gj[:], T.gs[:], W - 1, None, Alu.bitwise_and, None, "gs", gm)
+        tt(T.e2[:], T.e2[:], T.LN[:, 16:32], Alu.mult, "e2 lrn", "e2")
+        if not last:
+            cp(T.gu[:], gj[:], gm, "gu")
+        else:
+            ts(T.g16[:], gj[:], -2048.0, None, Alu.add, None, gm, "g16")
+        tt(T.e2[:], T.e2[:], T.OL[:, 0:16], Alu.add, "e2 OL", "e2")
+        cp(T.ccf[:], T.ccu[:], "ccu", "ccf")
+        ts(T.mou[:], T.e2[:], 2048.0, None, Alu.add, None, "e2", "mou")
+        tt(T.tt[:], P[6][:, 256:512], T.cc16[:], Alu.subtract, "cc16 P6", "tt")
+        tt(T.dA[:], Xw.indirect(T.mou[:]), T.A[:], Alu.subtract, "X mou A", "dA")
+        dedupe_b(16)
+        onehot(128, 2)
+        mm(P[2][:, 0:L], T.Id[:], T.dA[:], True, False, "Id dA", "P2")
+        mm(P[2][:, 0:L], T.Id2[:], T.A[:], False, False, "Id2 A", "P2")
+        for s in range(16):
+            mm(P[2][:, s:L:16], T.Bc[:, 128 * s:128 * s + 128], T.LB[:, 0:16], False, s == 15, "Bc LB", "P2")
+        for h, (I_, inm) in enumerate(((T.Id, "Id"), (T.Idm, "Idm"))):
+            mm(P[3][:, L * h:L * h + L], I_[:], T.dA[:], True, False, inm + " dA", "P3")
+            for s in range(16):
+                mm(P[3][:, L * h + s:L * h + L:16], T.Bc[:, 128 * s:128 * s + 128], T.LB[:, 16:32], False, s == 15, "Bc LB", "P3")
+        act(T.hA[:], P[2][:, 0:L], Act.Identity, "P2 " + CC, "hA", bias=BM, scale=0.4995)
+        act(T.r23[:], P[3][:], Act.Relu, "P3", "r23")
+        act(T.avg[:], T.hA[:], Act.Relu, "hA " + CC, "avg", bias=BMN)
+        if not last:
+            options_first()
+        write_cols(16, T.ccf, "ccf")
+        mm(P[0][:, 0:L], T.Id[:], T.r23[:, 0:L], True, False, "Id r23", "P0")
+        mm(P[0][:, 0:L], T.Id[:], T.r23[:, L:512], False, False, "Id r23", "P0")
+        mm(P[0][:, 0:L], T.Id[:], T.avg[:], False, True, "Id avg", "P0")
+        if not last:
+            act(T.A[:], P[0][:, 0:L], Act.Copy, "P0", "A")
+            act(T.nA[:, NX:L], P[0][:, NX:L], Act.Identity, "P0", "nA", scale=-1.0)
+            gate_patterns()
+        else:
+            act(T.yao[:], P[0][:, 0:L], Act.Copy, "P0", "yao")
+            dma("s", T.ya[:], T.yao[:], "yao", "out0")
+            for s in range(16):
+                mm(P[1][0:8, s:L:16], T.Bc[:, 128 * s:128 * s + 128:16], T.g16[:], True, True, "Bc g16", "P1")
+            ts(T.ygo[0:8, :], P[1][0:8, 0:L], 2048.0, None, Alu.add, None, "P1", "ygo")
+            dma("s", T.yg[:], T.ygo[0:8, :], "ygo", "out1")
+        ts(T.au[:, 0:6], Rt[:, 0:24:4], 2048.0, None, Alu.add, None, rn, "au")
+        ts(T.e1[:, 0:6], Rt[:, 0:24:4], -3000.0, R2B, Alu.is_lt, Alu.mult, rn + " " + CC, "e1")
+        cp(T.Xa[:], Xw.indirect(T.au[:, 0:6]), "X au", "Xa")
+        cp(T.c3u[:], Iw.indirect(T.au[:, 0:6]), "It au", "c3u")
+        for p in range(6):
+            act(T.Xar[:, p::16], T.Xa[:], Act.Copy, "Xa", "Xar_a")
+        for p in range(6, 16):
+            cp(T.Xar[:, p::16], T.Xa[:], "Xa", "Xar_v")
+        tt(T.base[:, 0:6], T.e1[:, 0:6], Rt[:, 0:24:4], Alu.add, "e1 " + rn, "base")
+        ts(T.b16[:, 0:6], Rt[:, 1:24:4], -8192.0, None, Alu.add, None, rn, "b16")
+        for u in range(3):
+            o = 512 * u
+            tt(T.d2[:, o:o + 512], Xw.indirect(T.c3u[:, 32 * u:32 * u + 32]), T.Xar[:, o:o + 512], Alu.subtract,
+               "X c3u Xar_a Xar_v", "d20 d21" if u == 0 else "d3%d" % u)
+            act(T.a2[:, o:o + 512], T.d2[:, o:o + 512], Act.Abs, "d20" if u == 0 else "d3%d" % u, "a20 a21" if u == 0 else "a3%d" % u)
+            if u == 0:
+                dedupe_a(6)
+                rep(6, 0, CAP, T.b16[:, 0:6], "b16")
+        farthest(CAP, 1, ["a20 a31 a32"])
+        ts(T.c316[:], T.c3u[:], -2048.0, None, Alu.add, None, "c3u", "c316")
+        cp(T.c3f[:], T.c3u[:], "c3u", "c3f")
+        tt(T.tt[:, 0:CAP], P[6][:, 0:CAP], T.c316[:], Alu.subtract, "c316 P6", "tt")
+        dedupe_b(6)
+        if not last:
+            arep()
+        else:
+            ts(T.Yw[:], T.Ff[:], G15, RP1, Alu.is_equal, Alu.mult, "Ff " + CC, "Yw")
+            ts(T.Yh[:], T.Ff[:], G15, RP1, Alu.is_equal, Alu.mult, "Ff " + CC, "Yh")
+        onehot(CAP, 1)
+        write_cols(6, T.c3f, "c3f")
+    n16 = 16 - NF32
+    half = n16 // 2
+    for a, b, nm in ((0, half, "Ih0"), (half, n16, "Ih1")):
+        ts(T.Ih[:, 256 * a:256 * b], T.It[:, 256 * (NF32 + a):256 * (NF32 + b)], -2048.0, None, Alu.add, None, "It", nm)
+    for s in range(16):
+        if s < NF32:
+            mm(P[1][:, 256:512], T.Yw[:, 15 - s:143 - s], T.It[:, 256 * s:256 * s + 256], s == 0, False, "Yw It", "P1")
+        else:
+            a = s - NF32
+            mm(P[1][:, 256:512], T.Yh[:, 15 - s:143 - s], T.Ih[:, 256 * a:256 * a + 256], False, s == 15,
+               "Yh " + ("Ih0" if a < half else "Ih1"), "P1")
+    ts(T.yco[:], P[1][:, 256:512], YB, None, Alu.add, None, "P1 " + CC, "yco")
+    dma("s", T.yc[:], T.yco[:], "yco", "out2")
+    op("s", lambda: None, "out0 out1 out2 sent", "")
+    schedule(g, T, ops)

@@ -2,7 +2,10 @@ from concourse.bass import DstId, RemoteDMATransfer
 from concourse.mybir import dt, AluOpType, AxisListType, ActivationFunctionType
 
 W, L, RO, CAP = 4096, 256, 3, 96
-NX = 128
+NX = 96
+NV2 = 0
+HOOKQ = 15
+RB = (2, 3, 6, 7)
 NF32 = 6
 PARTS = {"c_", "Bc", "Arep", "Rs", "Xcr", "CK", "C16", "OH", "Xar_a", "Xar_v", "d2o"}
 F32, BF, F16, I32, U16 = "float32", "bfloat16", "float16", "int32", "uint16"
@@ -24,7 +27,7 @@ _sb(F32, It=IW, Ff=144, FK=128, Gm=128, col=16, rowm=16, thf=4, thc=4, E8=128, Y
     hA=L, yao=L, ygo=L, yco=L, c3f=CAP)
 _sb(BF, X=W, A=L, nA=L, Arep=16 * NX, Xc=L, Xcr=W, dd=48 * NX, rr=48 * NX, ab=48 * (L - NX), d2=W, a2=W,
     Bc=2048, Dm=2048, Sa=144, Sb=144, Sm=144, Rs=432, Q=144, Id=128, Id2=128, Idm=128, BO=128, Uu=128, Tm=128,
-    Rk=128, On=128, W16=8, TBK=L, rst=L, RS=L, c75=16, Yh=144, NR0=192, NR1=192, EQ0=512, EQ1=512, e2b=64,
+    Rk=128, On=128, W16=8, TBK=L, rst=L, RS=L, c75=16, Yh=144, NR0=192, NR1=192, EQ=2048, e2b=64,
     LN=32, LB=32, Pq=16, OH=L, dA=L, r23=512, avg=L, Xa=CAP, Xar=16 * CAP)
 _sb(F16, OPT=L, C16=768, cc16=L, A8a=512, A8b=512, FN=768, FS=512, AM=32, dumx=16, b16=16, key=16, g16=16,
     c316=CAP, Ih=W - 256 * NF32)
@@ -55,7 +58,7 @@ def schedule(g, T, ops):
             for j in prev:
                 same = ops[j]["e"] == e and ops[j]["sem"] is None and not asyn
                 part = j == lastw.get(r) and (r in PARTS or r.startswith("ab"))
-                if j != i and (not same or (e != "p" and not r[1:].isdigit() and not part)):
+                if j != i and (not same or (e != "p" and not (r[0] == "P" and r[1:].isdigit()) and not part)):
                     deps.add(j)
         w = []
         if o["f"] is not None:
@@ -276,13 +279,17 @@ def program(g, core, T0, topo):
         ts(T.OPT[:], T.TB[:, 0:W].indirect(T.gu[:]), -2048.0, None, Alu.add, None, TBall + " gu", "OPT")
         for u in range(4):
             mm(P[5][:, 0:64], T.Q[:, 12 - 4 * u:140 - 4 * u], T.OPT[:, u::4], u == 0, u == 3, "Q OPT", "P5")
+
+    def options_list():
         ts(T.clu[:], P[5][:, 0:64], 2048.0, None, Alu.add, None, "P5", "clu")
 
-    def options_rest(gi, gn):
+    def options_turn():
         for k in range(3):
             for s in range(16):
                 mm(P[5][:, 64 + 16 * k:80 + 16 * k], T.Rs[:, 144 * k + 15 - s:144 * k + 143 - s], T.OPT[:, s::16],
                    s == 0, s == 15, "Rs OPT", "P5")
+
+    def options_rest(gi, gn):
         ts(T.t1[:], gi[:], 1, None, Alu.bitwise_and, None, gn, "t1")
         ts(T.cm[:], gi[:], -2048.0, None, Alu.add, None, gn, "cm")
         ts(T.t2[:], T.t1[:], -2.0, 1.0, Alu.mult, Alu.add, "t1", "t2")
@@ -316,6 +323,8 @@ def program(g, core, T0, topo):
 
     def t1v(c, k):
         e, lo, n, c0 = segs(c)[0]
+        if e != "v":
+            return
         o = 48 * lo + 16 * n * k
         nm = "dd%d%d" % (c, k)
         tt(T.dd[:, o:o + 16 * n], Xw.indirect(T.CK[:, 256 * k + lo:256 * k + lo + n]), T.Arep[:, 16 * lo:16 * (lo + n)],
@@ -349,7 +358,7 @@ def program(g, core, T0, topo):
                 mm(P[b][:, o:o + n], T.BO[:], rhs, True, True, "BO NR%d" % b, "P%d" % b)
 
     def rot(c, j):
-        b = 2 + j % 2
+        b = RB[j]
         for i in range(4):
             s = 4 * j + i
             for h in range(2):
@@ -368,23 +377,25 @@ def program(g, core, T0, topo):
         for n in (64, 128, 256):
             cp(A8[:, n:2 * n], A8[:, 0:n], an, an)
 
-    def member(c):
+    def member(c, after={}):
         b = c % 2
         A8, an = (T.A8a, "A8a") if b == 0 else (T.A8b, "A8b")
         for j in range(4):
-            EQ = T0["EQ%d" % (j % 2)]
-            tt(EQ[:], A8[:], P[2 + j % 2][:], Alu.is_equal, an + " P%d" % (2 + j % 2), "EQ%d" % (j % 2))
-            if j < 2:
-                rot(c, j + 2)
-            elif c < 3:
-                rot(c + 1, j - 2)
+            o = 512 * j
+            tt(T0.EQ[:, o:o + 512], A8[:], P[RB[j]][:], Alu.is_equal, an + " P%d" % RB[j], "EQ%d" % j)
             for i in range(4):
-                mm(P[4][:, 0:128], T.Id[:], EQ[:, 128 * i:128 * i + 128], j == 0 and i == 0, j == 3 and i == 3,
-                   "Id EQ%d" % (j % 2), "P4")
+                mm(P[4][:, 0:128], T.Id[:], T0.EQ[:, o + 128 * i:o + 128 * i + 128], j == 0 and i == 0, j == 3 and i == 3,
+                   "Id EQ%d" % j, "P4")
             if j == 0:
                 for h in range(2):
                     o = 256 * (h + 1) + 64 * c
                     mm(P[4][:, 64 * h:64 * h + 64], T.Id[:], T.FN[:, o:o + 64], False, False, "Id FN%d%d" % (c, h + 1), "P4")
+            if c < 3 and j < 2:
+                rot(c + 1, j)
+            if j in after:
+                after[j]()
+        if c < 3:
+            late.append(c + 1)
 
     def okrows(c):
         b = c % 2
@@ -394,17 +405,35 @@ def program(g, core, T0, topo):
         tt(T.FS[:, o:o + 64], T.e2b[:], P[4][:, 0:64], Alu.min, "e2b P4", "FSo%d" % c)
         mm(P[4][:, 256:320], T.Id[:], A8[:, 0:64], True, False, "Id " + an, "P4")
         mm(P[4][:, 256:320], T.Tm[:], T.FS[:, o:o + 64], False, True, "Tm FSo%d" % c, "P4")
+        if late:
+            c1 = late.pop()
+            rot(c1, 2)
+            rot(c1, 3)
 
     def selrow(c):
         ts(T.FS[:, 64 * c:64 * c + 64], P[4][:, 256:320], -8192.0, -2048.0, Alu.add, Alu.max, "P4", "FSs%d" % c)
 
     def s2gather(u):
         o = 1024 * u
-        tt(T.d2[:, o:o + 1024], Xw.indirect(T.ccu[:, 64 * u:64 * u + 64]), T.Xcr[:, o:o + 1024], Alu.subtract, "X ccu Xcr", "d2%d" % u)
+        tt(T.d2[:, o:o + 1024], Xw.indirect(T.ccu[:, 64 * u:64 * u + 64]), T.Xcr[:, o:o + 1024], Alu.subtract, "X ccu Xcr",
+           "d2%d d2%d" % (2 * u, 2 * u + 1))
 
     def s2abs(u):
         o = 1024 * u
-        act(T.a2[:, o:o + 1024], T.d2[:, o:o + 1024], Act.Abs, "d2%d" % u, "a2%d" % u)
+        act(T.a2[:, o:o + 1024], T.d2[:, o:o + 1024], Act.Abs, "d2%d" % (2 * u), "a2%d a2%d" % (2 * u, 2 * u + 1))
+
+    def s2fetch(i):
+        if i < 8:
+            act(T.d2[:, 512 * i:512 * i + 512], Xw.indirect(T.ccu[:, 32 * i:32 * i + 32]), Act.Copy, "X ccu", "d2%d" % i)
+
+    def s2piece(i):
+        o = 512 * i
+        mm(P[0][:], T.Id[:], T.d2[:, o:o + 512], True, False, "Id d2%d" % i, "P0")
+        mm(P[0][:], T.Idm[:], T.Xcr[:, o:o + 512], False, True, "Idm Xcr", "P0")
+        s2fetch(i + 1)
+        act(T.a2[:, o:o + 512], P[0][:], Act.Abs, "P0", "a2%d" % i)
+
+    late = []
 
     def farthest(n, halves, r):
         w = 128 * halves
@@ -437,14 +466,17 @@ def program(g, core, T0, topo):
         tt(T.e2[:, 0:nq], T.e1[:, 0:nq], T.base[:, 0:nq], Alu.add, "e1 base", "e2")
         ts(T.ou[:, 0:2 * nq:2], T.e2[:, 0:nq], 2048.0, None, Alu.add, None, "e2", "ou")
 
-    def write_cols(nq, cf, cn):
+    def write_cols(nq, cf, cn, hook=None):
         n = 16 * nq
         tt(T.tu[:, 0:n], T.tt[:, 0:n], P[7][:, 256:256 + n], Alu.mult, "tt P7", "tu")
         for q in reversed(range(nq)):
+            if hook and q == HOOKQ:
+                hook()
             tt(Iw.indirect(T.ou[:, 2 * q:2 * q + 1]), cf[:, 16 * q:16 * q + 16], T.tu[:, 16 * q:16 * q + 16], Alu.add,
                "ou tu " + cn, "It")
 
     options_first()
+    options_list()
     gate_patterns()
     for t in range(RO):
         gi, gn = T0["gi%d" % (t % 2)], "gi%d" % (t % 2)
@@ -456,6 +488,7 @@ def program(g, core, T0, topo):
         asegs = [(c, s) for c in range(4) for s in segs(c) if s[0] == "a"]
         for c, s in asegs:
             t1a(s[1], s[2])
+        options_turn()
         cp(T.CU[:, 0:4 * NX], Iw.indirect(T.clu[:, 0:NX // 4]), "It clu", "CUv")
         for k in range(3):
             cp(T.CK[:, 256 * k:256 * k + NX], T.CU[:, k:4 * NX:4], "CUv", "CK")
@@ -467,53 +500,60 @@ def program(g, core, T0, topo):
         tt(T.d10[:], T.C16[:, 256:512], T.C16[:, 0:256], Alu.subtract, "C16", "d10")
         t1v(1, 0)
         near(0, t)
-        rot(0, 0)
-        rot(0, 1)
+        for j in range(4):
+            rot(0, j)
         t1v(1, 1)
         t1v(1, 2)
         for c, s in asegs:
             if c == 1:
                 suma(c, s[1], s[2], s[3])
         first_col(0)
+        a3 = [s for c, s in asegs if c == 3]
+        piece = [2 * NV2]
+
+        def s2next():
+            if piece[0] < 8:
+                s2piece(piece[0])
+                piece[0] += 1
+        near(1, t)
         cp(T.ccu[:], Iw.indirect(T.gu[:]), "It gu", "ccu")
+        member(0)
+        first_col(1)
         for c, s in asegs:
             if c == 2:
                 suma(c, s[1], s[2], s[3])
-        member(0)
-        near(1, t)
         okrows(0)
-        s2gather(0)
-        first_col(1)
-        selrow(0)
         near(2, t)
+        selrow(0)
         member(1)
         first_col(2)
-        okrows(1)
-        s2gather(1)
-        selrow(1)
-        a3 = [s for c, s in asegs if c == 3]
         for s in a3[:-1]:
             suma(3, s[1], s[2], s[3])
-        member(2)
-        okrows(2)
-        suma(3, a3[-1][1], a3[-1][2], a3[-1][3])
-        s2gather(2)
-        selrow(2)
-        near(3, t)
+        okrows(1)
         ts(T.cc16[:], T.ccu[:], -2048.0, None, Alu.add, None, "ccu", "cc16")
+        for u in range(NV2):
+            s2gather(u)
+        selrow(1)
+        s2fetch(piece[0])
+        member(2, {1: lambda: suma(3, a3[-1][1], a3[-1][2], a3[-1][3]), 2: s2next})
+        near(3, t)
+        okrows(2)
+        s2next()
         first_col(3)
-        for u in range(3):
-            s2abs(u)
+        selrow(2)
         FNall = " ".join("FN%d%d" % (c, k) for c in range(4) for k in range(3))
-        member(3)
-        for s in range(16):
-            mm(P[5][:, 160:208], T.Sa[:, 15 - s:143 - s], T.FN[:, s::16], s == 0, s == 15, "Sa " + FNall, "P5")
+
+        def survivors():
+            for s in range(16):
+                mm(P[5][:, 160:208], T.Sa[:, 15 - s:143 - s], T.FN[:, s::16], s == 0, s == 15, "Sa " + FNall, "P5")
+        member(3, {0: s2next, 1: survivors, 2: s2next})
         okrows(3)
         ts(T.Nn[:], P[5][:, 160:208], -1.0 / 16, 1.0, Alu.mult, Alu.add, "P5", "Nn")
         selrow(3)
         FSall = " ".join("FS%s%d" % (x, c) for c in range(4) for x in "so")
         for s in range(16):
             mm(P[5][:, 128:160], T.Sa[:, 15 - s:143 - s], T.FS[:, s::16], s == 0, s == 15, "Sa " + FSall, "P5")
+        s2next()
         tt(T.la[:], T.Nn[:, 0:16], T.Nn[:, 16:32], Alu.add, "Nn", "la")
         tt(T.x2[:], T.Nn[:, 0:32], T.d2o[:], Alu.mult, "Nn d2o", "x2")
         tt(T.la[:], T.la[:], T.Nn[:, 32:48], Alu.add, "la Nn", "la")
@@ -535,7 +575,7 @@ def program(g, core, T0, topo):
         mm(P[5][:, 224:240], T.BO[:], T.Pq[:], False, False, "BO Pq", "P5")
         mm(P[5][:, 224:240], T.Id[:], T.dumx[:], False, True, "Id dumx", "P5")
         mm(P[5][:, 240:241], T.On[:], T.Pq[:, 15:16], True, True, "On Pq", "P5")
-        act(T.LB[:], T.LN[:], Act.Identity, "lrn nl", "LB", scale=-1024.0)
+        s2next()
         tt(T.ww[:], T.pre[:], T.hh[:], Alu.mult, "pre hh", "ww")
         tt(T.AM[:, 16:32], T.ww[:], T.mdef[:], Alu.add, "ww mdef", "m16")
         ts(T.mi[:], T.AM[:, 16:32], 2048.0, None, Alu.add, None, "m16", "mi")
@@ -546,6 +586,7 @@ def program(g, core, T0, topo):
         ts(T.offu[:], T.offf[:], PAR, None, Alu.add, None, "offf " + CC, "offu")
         tt(T.AM[:, 0:16], T.t2[:], T.AM[:, 16:32], Alu.add, "t2 m16", "a16")
         rep(6, 0, 512, T.AM[:], "a16 m16")
+        s2next()
         ts(T.c37e[:], T.c37[:], P[5][:, 240:241], None, Alu.add, None, "c37 P5", "c37e")
         tt(T.mc[:], T.mi[:], gi[:], Alu.mult, "mi " + gn, "mc")
         tt(T.e1[:], T.LN[:, 0:16], T.ddm[:], Alu.mult, "nl ddm", "e1")
@@ -563,10 +604,13 @@ def program(g, core, T0, topo):
         op("g", lambda St=St, Rt=Rt, t=t, pid=pid, rid=rid, mask=mask:
            g.remote_dma(Rt[:], St[:], T.sem["arr%d" % t], T.sem.snt, pid, rid, mask), sn, "sent", sem="snt", n=len(eng))
         op("g", None, "", rn, sem="arr%d" % t, n=len(topo.engines(src, core)[::2]))
-        s2gather(3)
-        s2abs(3)
-        farthest(128, 2, ["a20 a21", "a22 a23"])
         dedupe_a(16)
+        for u in range(8):
+            s2next()
+        for u in range(NV2):
+            s2abs(u)
+        farthest(128, 2, ["a20 a21 a22 a23", "a24 a25 a26 a27"])
+        act(T.LB[:], T.LN[:], Act.Identity, "lrn nl", "LB", scale=-1024.0)
         tt(T.gs[:], T.sh[:], T.c37e[:], Alu.add, "sh c37e", "gs")
         tt(T.e2[:], T.AM[:, 16:32], T.OL[:, 0:16], Alu.subtract, "m16 OL", "e2")
         ts(gj[:], T.gs[:], W - 1, None, Alu.bitwise_and, None, "gs", gm)
@@ -576,12 +620,11 @@ def program(g, core, T0, topo):
         else:
             ts(T.g16[:], gj[:], -2048.0, None, Alu.add, None, gm, "g16")
         tt(T.e2[:], T.e2[:], T.OL[:, 0:16], Alu.add, "e2 OL", "e2")
-        cp(T.ccf[:], T.ccu[:], "ccu", "ccf")
-        ts(T.mou[:], T.e2[:], 2048.0, None, Alu.add, None, "e2", "mou")
         tt(T.tt[:], P[6][:, 256:512], T.cc16[:], Alu.subtract, "cc16 P6", "tt")
+        ts(T.mou[:], T.e2[:], 2048.0, None, Alu.add, None, "e2", "mou")
+        if not last:
+            options_first()
         tt(T.dA[:], Xw.indirect(T.mou[:]), T.A[:], Alu.subtract, "X mou A", "dA")
-        dedupe_b(16)
-        onehot(128, 2)
         mm(P[2][:, 0:L], T.Id[:], T.dA[:], True, False, "Id dA", "P2")
         mm(P[2][:, 0:L], T.Id2[:], T.A[:], False, False, "Id2 A", "P2")
         for s in range(16):
@@ -594,15 +637,23 @@ def program(g, core, T0, topo):
         act(T.r23[:], P[3][:], Act.Relu, "P3", "r23")
         act(T.avg[:], T.hA[:], Act.Relu, "hA " + CC, "avg", bias=BMN)
         if not last:
-            options_first()
-        write_cols(16, T.ccf, "ccf")
+            options_list()
+        dedupe_b(16)
+        cp(T.ccf[:], T.ccu[:], "ccu", "ccf")
+        onehot(128, 2)
+
+        def came(Rt=Rt, rn=rn):
+            ts(T.au[:, 0:6], Rt[:, 0:24:4], 2048.0, None, Alu.add, None, rn, "au")
+            act(T.Xa[:], Xw.indirect(T.au[:, 0:6]), Act.Copy, "X au", "Xa")
+            for p in range(16):
+                act(T.Xar[:, p::16], T.Xa[:], Act.Copy, "Xa", "Xar_a")
+        write_cols(16, T.ccf, "ccf", came)
         mm(P[0][:, 0:L], T.Id[:], T.r23[:, 0:L], True, False, "Id r23", "P0")
         mm(P[0][:, 0:L], T.Id[:], T.r23[:, L:512], False, False, "Id r23", "P0")
         mm(P[0][:, 0:L], T.Id[:], T.avg[:], False, True, "Id avg", "P0")
         if not last:
             act(T.A[:], P[0][:, 0:L], Act.Copy, "P0", "A")
             act(T.nA[:, NX:L], P[0][:, NX:L], Act.Identity, "P0", "nA", scale=-1.0)
-            gate_patterns()
         else:
             act(T.yao[:], P[0][:, 0:L], Act.Copy, "P0", "yao")
             dma("s", T.ya[:], T.yao[:], "yao", "out0")
@@ -610,25 +661,25 @@ def program(g, core, T0, topo):
                 mm(P[1][0:8, s:L:16], T.Bc[:, 128 * s:128 * s + 128:16], T.g16[:], True, True, "Bc g16", "P1")
             ts(T.ygo[0:8, :], P[1][0:8, 0:L], 2048.0, None, Alu.add, None, "P1", "ygo")
             dma("s", T.yg[:], T.ygo[0:8, :], "ygo", "out1")
-        ts(T.au[:, 0:6], Rt[:, 0:24:4], 2048.0, None, Alu.add, None, rn, "au")
-        ts(T.e1[:, 0:6], Rt[:, 0:24:4], -3000.0, R2B, Alu.is_lt, Alu.mult, rn + " " + CC, "e1")
-        cp(T.Xa[:], Xw.indirect(T.au[:, 0:6]), "X au", "Xa")
         cp(T.c3u[:], Iw.indirect(T.au[:, 0:6]), "It au", "c3u")
-        for p in range(6):
-            act(T.Xar[:, p::16], T.Xa[:], Act.Copy, "Xa", "Xar_a")
-        for p in range(6, 16):
-            cp(T.Xar[:, p::16], T.Xa[:], "Xa", "Xar_v")
-        tt(T.base[:, 0:6], T.e1[:, 0:6], Rt[:, 0:24:4], Alu.add, "e1 " + rn, "base")
-        ts(T.b16[:, 0:6], Rt[:, 1:24:4], -8192.0, None, Alu.add, None, rn, "b16")
-        for u in range(3):
+        act(T.d2[:, 1024:1536], Xw.indirect(T.c3u[:, 64:96]), Act.Copy, "X c3u", "d22")
+        ts(T.e1[:, 0:6], Rt[:, 0:24:4], -3000.0, R2B, Alu.is_lt, Alu.mult, rn + " " + CC, "e1")
+        mm(P[1][:], T.Id[:], T.d2[:, 1024:1536], True, False, "Id d22", "P1")
+        mm(P[1][:], T.Idm[:], T.Xar[:, 1024:1536], False, True, "Idm Xar_a", "P1")
+        for u in range(2):
             o = 512 * u
             tt(T.d2[:, o:o + 512], Xw.indirect(T.c3u[:, 32 * u:32 * u + 32]), T.Xar[:, o:o + 512], Alu.subtract,
-               "X c3u Xar_a Xar_v", "d20 d21" if u == 0 else "d3%d" % u)
-            act(T.a2[:, o:o + 512], T.d2[:, o:o + 512], Act.Abs, "d20" if u == 0 else "d3%d" % u, "a20 a21" if u == 0 else "a3%d" % u)
+               "X c3u Xar_a", "d2%d" % u)
+            act(T.a2[:, o:o + 512], T.d2[:, o:o + 512], Act.Abs, "d2%d" % u, "a2%d" % u)
             if u == 0:
+                act(T.a2[:, 1024:1536], P[1][:], Act.Abs, "P1", "a22")
+                tt(T.base[:, 0:6], T.e1[:, 0:6], Rt[:, 0:24:4], Alu.add, "e1 " + rn, "base")
+                ts(T.b16[:, 0:6], Rt[:, 1:24:4], -8192.0, None, Alu.add, None, rn, "b16")
                 dedupe_a(6)
                 rep(6, 0, CAP, T.b16[:, 0:6], "b16")
-        farthest(CAP, 1, ["a20 a31 a32"])
+        farthest(CAP, 1, ["a20 a21 a22"])
+        if not last:
+            gate_patterns()
         ts(T.c316[:], T.c3u[:], -2048.0, None, Alu.add, None, "c3u", "c316")
         cp(T.c3f[:], T.c3u[:], "c3u", "c3f")
         tt(T.tt[:, 0:CAP], P[6][:, 0:CAP], T.c316[:], Alu.subtract, "c316 P6", "tt")

@@ -3,11 +3,13 @@ from concourse.mybir import dt, AluOpType, AxisListType, ActivationFunctionType
 
 W, L, RO, CAP = 4096, 256, 3, 96
 NX = 96
-NV2 = 0
+NV2 = 1
 HOOKQ = 15
 RB = (2, 3, 6, 7)
-NF32 = 6
-PARTS = {"c_", "Bc", "Arep", "Rs", "Xcr", "CK", "C16", "OH", "Xar_a", "Xar_v", "d2o"}
+NF32 = 4
+XV, AG = 8, 16
+PARTS = {"Areg", "c_", "Bc", "Arep", "Rs", "Xcr", "CK", "C16", "OH", "Xar_a", "Xar_v", "d2o"}
+CYC, PCYC, VFIX, AFIX, HOP, SELF, LOOK = 0.92, 0.47, 30.0, 50.0, 150.0, 70.0, 60.0
 F32, BF, F16, I32, U16 = "float32", "bfloat16", "float16", "int32", "uint16"
 IW = W + 32
 
@@ -101,6 +103,72 @@ def schedule(g, T, ops):
                 ins.then_inc(T.sem[s], 1)
 
 
+def reorder(ops):
+    n = len(ops)
+    lastw, readers, lastq = {}, {}, {}
+    pre = []
+    for i, o in enumerate(ops):
+        d = set(lastw[r] for r in o["r"] if r in lastw)
+        for r in o["w"]:
+            d.update(readers.get(r, []))
+            if r in lastw:
+                d.add(lastw[r])
+        if o["e"] in "gs" or o["sem"] is not None:
+            if o["e"] in lastq:
+                d.add(lastq[o["e"]])
+            lastq[o["e"]] = i
+        d.discard(i)
+        pre.append(d)
+        for r in o["r"]:
+            readers.setdefault(r, []).append(i)
+        for r in o["w"]:
+            lastw[r] = i
+            readers[r] = []
+
+    def gap(j, i):
+        a, b = ops[j], ops[i]
+        if a["sem"] is not None:
+            return a["lat"] if set(a["w"]) & set(b["r"]) or b["f"] is None else 0
+        if a["e"] != b["e"]:
+            return HOP
+        return SELF if set(a["w"]) & set(b["r"]) or (a["e"] == "v" and "It" in b["w"]) else 0
+
+    succ = [[] for _ in ops]
+    for i in range(n):
+        for j in pre[i]:
+            succ[j].append((i, gap(j, i)))
+    way = [0.0] * n
+    for i in reversed(range(n)):
+        way[i] = ops[i]["c"] + max([x + way[k] for k, x in succ[i]] + [0])
+    left = [len(p) for p in pre]
+    ready = {e: [] for e in "vapgs"}
+    at = [0.0] * n
+    for i in range(n):
+        if not left[i]:
+            ready[ops[i]["e"]].append(i)
+    free = {e: 0.0 for e in ready}
+    order = []
+    while len(order) < n:
+        best = None
+        for e in ready:
+            if ready[e]:
+                t0 = max(free[e], min(at[i] for i in ready[e]))
+                if best is None or t0 < best[0]:
+                    best = (t0, e)
+        t0, e = best
+        i = max((k for k in ready[e] if at[k] <= t0 + LOOK), key=lambda k: (way[k], -k))
+        ready[e].remove(i)
+        st = max(t0, at[i])
+        free[e] = st + ops[i]["c"]
+        order.append(i)
+        for k, x in succ[i]:
+            at[k] = max(at[k], free[e] + x)
+            left[k] -= 1
+            if not left[k]:
+                ready[ops[k]["e"]].append(k)
+    return [ops[i] for i in order]
+
+
 def rank_program(g, core, T, topo):
     if T.rank_of(core) is not None:
         program(g, core, T, topo)
@@ -142,33 +210,52 @@ def program(g, core, T0, topo):
     def un(x):
         return x[0] if isinstance(x, list) else x
 
-    def op(e, f, r, w, sem=None, n=0, inc=False):
+    def op(e, f, r, w, sem=None, n=0, inc=False, c=300.0, lat=0.0):
         r, w = names(r), names(w)
         banks = [x for x in r if x[0] == "P" and x[1:].isdigit()]
-        ops.append({"e": e, "f": f, "r": [x for x in r if x not in banks], "w": w + banks, "sem": sem, "n": n, "inc": inc})
+        ops.append({"e": e, "f": f, "r": [x for x in r if x not in banks], "w": w + banks, "sem": sem, "n": n, "inc": inc,
+                    "c": c, "lat": lat})
 
-    def dma(e, out, in_, r, w):
+    def dma(e, out, in_, r, w, lat=2500.0):
         q = {"s": g.sync, "a": g.scalar}[e]
-        op(e, lambda: q.dma_start(out, in_), r, w, sem="d%d" % nd[0], n=16, inc=True)
+        op(e, lambda: q.dma_start(out, in_), r, w, sem="d%d" % nd[0], n=16, inc=True, c=100.0, lat=lat)
         nd[0] += 1
 
+    def wide(x):
+        return "16" not in str(un(x).dtype)
+
+    def cost(out, ins, r, two=1.0, fix=VFIX):
+        r = set(names(r))
+        if r & {"ou", "offu"}:
+            return 50 + un(ins[0]).shape[1] * 3.8 * CYC
+        n = un(out).shape[1]
+        if r & {"X", "It", "TB0"} and r & {"gu", "clu", "CK", "CUa", "ccu", "c3u", "au", "mou"}:
+            return 60 + n * 1.56 * CYC
+        if any(x[0] == "P" and x[1:].isdigit() for x in r):
+            two = 1.0
+        elif not any(wide(x) for x in [out] + ins):
+            two *= 0.5
+        return fix + max(32, n * two) * CYC
+
     def ts(out, in0, s1, s2, o0, o1, r, w):
+        c = cost(out, [in0], r)
         if o1 is None:
-            op("v", lambda: V.tensor_scalar(un(out), un(in0), s1, None, o0), r, w)
+            op("v", lambda: V.tensor_scalar(un(out), un(in0), s1, None, o0), r, w, c=c)
         else:
-            op("v", lambda: V.tensor_scalar(un(out), un(in0), s1, s2, o0, o1), r, w)
+            op("v", lambda: V.tensor_scalar(un(out), un(in0), s1, s2, o0, o1), r, w, c=c)
 
     def tt(out, a, b, o, r, w):
-        op("v", lambda: V.tensor_tensor(un(out), un(a), un(b), o), r, w)
+        op("v", lambda: V.tensor_tensor(un(out), un(a), un(b), o), r, w, c=cost(out, [a, b], r, 2.0))
 
     def cp(out, a, r, w):
-        op("v", lambda: V.tensor_copy(un(out), un(a)), r, w)
+        op("v", lambda: V.tensor_copy(un(out), un(a)), r, w, c=cost(out, [a], r))
 
     def ms(out, c, w):
-        op("v", lambda: V.memset(out, c), "", w)
+        op("v", lambda: V.memset(out, c), "", w, c=cost(out, [], ""))
 
     def mm(out, l, rh, st, sp, r, w):
-        op("p", lambda: PE.matmul(out, l, rh, st, sp), r, w)
+        c = max(min(64, l.shape[1]), rh.shape[1]) * (4 if wide(rh) else 1) * PCYC
+        op("p", lambda: PE.matmul(out, l, rh, st, sp), r, w, c=c)
 
     def act(out, in_, fn, r, w, bias=None, scale=None):
         kw = {}
@@ -176,7 +263,7 @@ def program(g, core, T0, topo):
             kw["bias"] = bias
         if scale is not None:
             kw["scale"] = scale
-        op("a", lambda: S.activation(out, in_, fn, **kw), r, w)
+        op("a", lambda: S.activation(out, in_, fn, **kw), r, w, c=cost(out, [T.It[:]], r, 1.0, AFIX))
 
     def iota(out, pat, base, cm, w, small=True):
         if small:
@@ -192,14 +279,14 @@ def program(g, core, T0, topo):
     MAG16 = 201326592.0
 
     ms(T.TB[:], 0, "TB0")
-    dma("s", T.gi0[:], T.gate[:], "", "gi0")
-    for j in range(4):
-        dma("s", T.ic[:, 1024 * j:1024 * j + 1024], T.icol[:, 1024 * j:1024 * j + 1024], "", "ic%d" % j)
-    dma("a", T.A[:], T.acc0[:], "", "A")
+    dma("a", T.gi0[:], T.gate[:], "", "gi0")
     dma("a", T.thi[0:8, 0:3], T.th[:], "", "thi")
+    dma("a", T.A[:], T.acc0[:], "", "A")
+    for j in range(4):
+        dma("s", T.ic[:, 1024 * j:1024 * j + 1024], T.icol[:, 1024 * j:1024 * j + 1024], "", "ic%d" % j, 3500.0 + 2000 * j)
     for u in range(8):
-        dma("s", T.TB[16 * u:16 * u + 3, :], T.alt[3 * u:3 * u + 3, :], "TB0", "TB_%d" % u)
-    dma("s", T.X[:], T.pat[:], "", "X")
+        dma("s", T.TB[16 * u:16 * u + 3, :], T.alt[3 * u:3 * u + 3, :], "TB0", "TB_%d" % u, 7000.0)
+    dma("s", T.X[:], T.pat[:], "", "X", 10500.0)
     TBall = "TB0 " + " ".join("TB_%d" % u for u in range(8))
 
     iota(T.kc[:], [[0, 1]], 0, 1, "kc", small=False)
@@ -232,8 +319,9 @@ def program(g, core, T0, topo):
     cp(T.gu[:], T.gi0[:], "gi0", "gu")
     for s in range(16):
         act(T.Bc[:, 128 * s:128 * s + 128], T.BO[:], Act.Identity, "BO rowm", "Bc", scale=T.rowm[:, s:s + 1])
-    op("g", lambda: g.affine_select(T.Dm[:], T.Bc[:], [[0, 16], [-16, 8], [-1, 16]], Alu.not_equal, -1.0, 0, 1), "Bc", "Dm")
-    op("g", lambda: g.affine_select(T.Dm[:], T.Dm[:], [[-1, 16], [0, 8], [1, 16]], Alu.is_gt, 0.0, 0, 0), "Dm", "Dm")
+    op("g", lambda: g.affine_select(T.Dm[:], T.Bc[:], [[0, 16], [-16, 8], [-1, 16]], Alu.not_equal, -1.0, 0, 1), "Bc", "Dm",
+       c=3900.0)
+    op("g", lambda: g.affine_select(T.Dm[:], T.Dm[:], [[-1, 16], [0, 8], [1, 16]], Alu.is_gt, 0.0, 0, 0), "Dm", "Dm", c=3900.0)
     act(T.nA[:, NX:L], T.A[:, NX:L], Act.Identity, "A", "nA", scale=-1.0)
 
     def arep():
@@ -306,7 +394,7 @@ def program(g, core, T0, topo):
     def gate_patterns():
         act(T.Xc[:], Xw.indirect(T.gu[:]), Act.Copy, "X gu", "Xc")
         for p in range(16):
-            op("g", lambda p=p: g.affine_select(T.Xcr[:, p::16], T.Xc[:], [[0, L]], Alu.is_ge, 0.0, 0, 0), "Xc", "Xcr")
+            op("g", lambda p=p: g.affine_select(T.Xcr[:, p::16], T.Xc[:], [[0, L]], Alu.is_ge, 0.0, 0, 0), "Xc", "Xcr", c=650.0)
 
     def segs(c):
         lo, hi = 64 * c, 64 * c + 64
@@ -328,7 +416,7 @@ def program(g, core, T0, topo):
         o = 48 * lo + 16 * n * k
         nm = "dd%d%d" % (c, k)
         tt(T.dd[:, o:o + 16 * n], Xw.indirect(T.CK[:, 256 * k + lo:256 * k + lo + n]), T.Arep[:, 16 * lo:16 * (lo + n)],
-           Alu.subtract, "X CK Arep", nm)
+           Alu.subtract, "X CK Arep Areg", nm)
         ts(T.rr[:, o:o + 16 * n], T.dd[:, o:o + 16 * n], 0.0, None, Alu.max, None, nm, "r" + nm)
         b = c % 2
         for p in range(16):
@@ -339,7 +427,7 @@ def program(g, core, T0, topo):
     def t1a(lo, n):
         for l in range(lo, lo + n):
             o = 48 * (l - NX)
-            act(T.ab[:, o:o + 48], Xw.indirect(T.CU[:, 4 * l:4 * l + 3]), Act.Abs, "X CUa nA", "ab%d" % lo, bias=T.nA[:, l:l + 1])
+            act(T.ab[:, o:o + 48], Xw.indirect(T.CU[:, 4 * l:4 * l + 3]), Act.Abs, "X CUa nA", "abq ab%d" % lo, bias=T.nA[:, l:l + 1])
 
     def suma(c, lo, n, c0):
         o = 48 * (lo - NX)
@@ -420,7 +508,7 @@ def program(g, core, T0, topo):
 
     def s2abs(u):
         o = 1024 * u
-        act(T.a2[:, o:o + 1024], T.d2[:, o:o + 1024], Act.Abs, "d2%d" % (2 * u), "a2%d a2%d" % (2 * u, 2 * u + 1))
+        act(T.a2[:, o:o + 1024], T.d2[:, o:o + 1024], Act.Abs, "d2%d d2%d" % (2 * u, 2 * u + 1), "a2%d a2%d" % (2 * u, 2 * u + 1))
 
     def s2fetch(i):
         if i < 8:
@@ -443,10 +531,14 @@ def program(g, core, T0, topo):
                 mm(P[7][0:n, 128 * h + p:128 * h + 128:16], T.a2[:, 2048 * h + p:2048 * h + 16 * n:16], T.W16[:], False,
                    h == halves - 1 and p == 15, "W16 " + r[h], "P7")
 
-    def onehot(n, halves):
+    def onehot(n, halves, on_scalar=False):
         w = 128 * halves
         op("v", lambda: V.tensor_tensor_scan(T.SC[0:n, 0:w], T.rst[0:n, 0:w], P[7][0:n, 0:w], 0.0, Alu.mult, Alu.max), "rst P7", "SC")
-        for u in range(8 * halves):
+        if on_scalar:
+            ts(T.x2[:, 0:16], T.SC[:, 15:w:16], -1.0, 1.0, Alu.mult, Alu.add, "SC", "x2")
+            for u in range(8 * halves):
+                act(T.OH[:, 16 * u:16 * u + 16], P[7][:, 16 * u:16 * u + 16], Act.Relu, "x2 P7", "OH", bias=T.x2[:, u:u + 1])
+        for u in range(0 if on_scalar else 8 * halves):
             ts(T.OH[0:n, 16 * u:16 * u + 16], P[7][0:n, 16 * u:16 * u + 16], T.SC[0:n, 16 * u + 15:16 * u + 16], None,
                Alu.is_equal, None, "SC P7", "OH")
         for h in range(halves):
@@ -535,6 +627,7 @@ def program(g, core, T0, topo):
             s2gather(u)
         selrow(1)
         s2fetch(piece[0])
+        act(T.ccf[:], Iw.indirect(T.gu[:]), Act.Copy, "It gu", "ccf")
         member(2, {1: lambda: suma(3, a3[-1][1], a3[-1][2], a3[-1][3]), 2: s2next})
         near(3, t)
         okrows(2)
@@ -546,24 +639,26 @@ def program(g, core, T0, topo):
         def survivors():
             for s in range(16):
                 mm(P[5][:, 160:208], T.Sa[:, 15 - s:143 - s], T.FN[:, s::16], s == 0, s == 15, "Sa " + FNall, "P5")
-        member(3, {0: s2next, 1: survivors, 2: s2next})
-        okrows(3)
+        survivors()
+        member(3, {0: s2next})
         ts(T.Nn[:], P[5][:, 160:208], -1.0 / 16, 1.0, Alu.mult, Alu.add, "P5", "Nn")
+        okrows(3)
+        s2next()
+        tt(T.la[:], T.Nn[:, 0:16], T.Nn[:, 16:32], Alu.add, "Nn", "la")
+        tt(T.x2[:], T.Nn[:, 0:32], T.d2o[:], Alu.mult, "Nn d2o", "x2")
+        tt(T.la[:], T.la[:], T.Nn[:, 32:48], Alu.add, "la Nn", "la")
         selrow(3)
         FSall = " ".join("FS%s%d" % (x, c) for c in range(4) for x in "so")
         for s in range(16):
             mm(P[5][:, 128:160], T.Sa[:, 15 - s:143 - s], T.FS[:, s::16], s == 0, s == 15, "Sa " + FSall, "P5")
         s2next()
-        tt(T.la[:], T.Nn[:, 0:16], T.Nn[:, 16:32], Alu.add, "Nn", "la")
-        tt(T.x2[:], T.Nn[:, 0:32], T.d2o[:], Alu.mult, "Nn d2o", "x2")
-        tt(T.la[:], T.la[:], T.Nn[:, 32:48], Alu.add, "la Nn", "la")
         tt(T.lb[:], T.x2[:, 0:16], T.x2[:, 16:32], Alu.add, "x2", "lb")
         ts(T.one[:], T.la[:], 1.0, None, Alu.is_equal, None, "la", "one")
         ts(T.two[:], T.la[:], 1.5, None, Alu.is_gt, None, "la", "two")
         ts(T.none1[:], T.la[:], 1.0, None, Alu.not_equal, None, "la", "none1")
         tt(T.lb[:], T.lb[:], T.one[:], Alu.mult, "lb one", "lb")
-        tt(T.hh[:], T.two[:], P[5][:, 144:160], Alu.min, "two P5", "hh")
         tt(T.mdef[:], T.lb[:], T.OL[:, 32:48], Alu.add, "lb OL", "mdef")
+        tt(T.hh[:], T.two[:], P[5][:, 144:160], Alu.min, "two P5", "hh")
         tt(T.LN[:, 16:32], T.hh[:], T.one[:], Alu.add, "hh one", "lrn")
         tt(T.LN[:, 0:16], T.none1[:], T.hh[:], Alu.subtract, "none1 hh", "nl")
         tt(T.pre[:], P[5][:, 128:144], T.mdef[:], Alu.subtract, "mdef P5", "pre")
@@ -575,7 +670,6 @@ def program(g, core, T0, topo):
         mm(P[5][:, 224:240], T.BO[:], T.Pq[:], False, False, "BO Pq", "P5")
         mm(P[5][:, 224:240], T.Id[:], T.dumx[:], False, True, "Id dumx", "P5")
         mm(P[5][:, 240:241], T.On[:], T.Pq[:, 15:16], True, True, "On Pq", "P5")
-        s2next()
         tt(T.ww[:], T.pre[:], T.hh[:], Alu.mult, "pre hh", "ww")
         tt(T.AM[:, 16:32], T.ww[:], T.mdef[:], Alu.add, "ww mdef", "m16")
         ts(T.mi[:], T.AM[:, 16:32], 2048.0, None, Alu.add, None, "m16", "mi")
@@ -585,8 +679,17 @@ def program(g, core, T0, topo):
         ts(T.t2[:], T.t1[:], -2.0, 1.0, Alu.mult, Alu.add, "t1", "t2")
         ts(T.offu[:], T.offf[:], PAR, None, Alu.add, None, "offf " + CC, "offu")
         tt(T.AM[:, 0:16], T.t2[:], T.AM[:, 16:32], Alu.add, "t2 m16", "a16")
-        rep(6, 0, 512, T.AM[:], "a16 m16")
-        s2next()
+        rep(6, 0, L, T.AM[:, 0:16], "a16")
+        for u in range(8):
+            s2next()
+        for u in range(NV2):
+            s2abs(u)
+        farthest(128, 2, ["a20 a21 a22 a23", "a24 a25 a26 a27"])
+        mm(P[1][:, 0:L], T.Idm[:], T.cc16[:], True, False, "Idm cc16", "P1")
+        for s in range(16):
+            mm(P[1][:, s:L:16], T.Bc[:, 128 * s:128 * s + 128], T.AM[:, 16:32], False, s == 15, "Bc m16", "P1")
+        act(T.LB[:], T.LN[:], Act.Identity, "lrn nl", "LB", scale=-1024.0)
+        act(T.tt[:], P[1][:, 0:L], Act.Copy, "P1", "tt")
         ts(T.c37e[:], T.c37[:], P[5][:, 240:241], None, Alu.add, None, "c37 P5", "c37e")
         tt(T.mc[:], T.mi[:], gi[:], Alu.mult, "mi " + gn, "mc")
         tt(T.e1[:], T.LN[:, 0:16], T.ddm[:], Alu.mult, "nl ddm", "e1")
@@ -602,15 +705,11 @@ def program(g, core, T0, topo):
         eng = topo.engines(core, dst)[::2]
         mask = sum(1 << x for x in eng)
         op("g", lambda St=St, Rt=Rt, t=t, pid=pid, rid=rid, mask=mask:
-           g.remote_dma(Rt[:], St[:], T.sem["arr%d" % t], T.sem.snt, pid, rid, mask), sn, "sent", sem="snt", n=len(eng))
-        op("g", None, "", rn, sem="arr%d" % t, n=len(topo.engines(src, core)[::2]))
+           g.remote_dma(Rt[:], St[:], T.sem["arr%d" % t], T.sem.snt, pid, rid, mask), sn, "sent", sem="snt", n=len(eng),
+           c=500.0, lat=3000.0)
+        op("g", None, "", rn, sem="arr%d" % t, n=len(topo.engines(src, core)[::2]), c=0.0)
         dedupe_a(16)
-        for u in range(8):
-            s2next()
-        for u in range(NV2):
-            s2abs(u)
-        farthest(128, 2, ["a20 a21 a22 a23", "a24 a25 a26 a27"])
-        act(T.LB[:], T.LN[:], Act.Identity, "lrn nl", "LB", scale=-1024.0)
+        onehot(128, 2, True)
         tt(T.gs[:], T.sh[:], T.c37e[:], Alu.add, "sh c37e", "gs")
         tt(T.e2[:], T.AM[:, 16:32], T.OL[:, 0:16], Alu.subtract, "m16 OL", "e2")
         ts(gj[:], T.gs[:], W - 1, None, Alu.bitwise_and, None, "gs", gm)
@@ -620,34 +719,34 @@ def program(g, core, T0, topo):
         else:
             ts(T.g16[:], gj[:], -2048.0, None, Alu.add, None, gm, "g16")
         tt(T.e2[:], T.e2[:], T.OL[:, 0:16], Alu.add, "e2 OL", "e2")
-        tt(T.tt[:], P[6][:, 256:512], T.cc16[:], Alu.subtract, "cc16 P6", "tt")
         ts(T.mou[:], T.e2[:], 2048.0, None, Alu.add, None, "e2", "mou")
+        dedupe_b(16)
         if not last:
             options_first()
-        tt(T.dA[:], Xw.indirect(T.mou[:]), T.A[:], Alu.subtract, "X mou A", "dA")
+        act(T.dA[:], Xw.indirect(T.mou[:]), Act.Copy, "X mou", "dA")
         mm(P[2][:, 0:L], T.Id[:], T.dA[:], True, False, "Id dA", "P2")
-        mm(P[2][:, 0:L], T.Id2[:], T.A[:], False, False, "Id2 A", "P2")
+        mm(P[2][:, 0:L], T.Id[:], T.A[:], False, False, "Id A", "P2")
         for s in range(16):
             mm(P[2][:, s:L:16], T.Bc[:, 128 * s:128 * s + 128], T.LB[:, 0:16], False, s == 15, "Bc LB", "P2")
         for h, (I_, inm) in enumerate(((T.Id, "Id"), (T.Idm, "Idm"))):
             mm(P[3][:, L * h:L * h + L], I_[:], T.dA[:], True, False, inm + " dA", "P3")
+            mm(P[3][:, L * h:L * h + L], (T.Idm, T.Id)[h][:], T.A[:], False, False, "Id Idm A", "P3")
             for s in range(16):
                 mm(P[3][:, L * h + s:L * h + L:16], T.Bc[:, 128 * s:128 * s + 128], T.LB[:, 16:32], False, s == 15, "Bc LB", "P3")
+
+        def came(Rt=Rt, rn=rn):
+            ts(T.au[:, 0:6], Rt[:, 0:24:4], 2048.0, None, Alu.add, None, rn, "au")
+            act(T.Xa[:], Xw.indirect(T.au[:, 0:6]), Act.Copy, "X au", "Xa")
+            for p in range(XV):
+                cp(T.Xar[:, p::16], T.Xa[:], "Xa", "Xar_v")
+            for p in range(XV, 16):
+                act(T.Xar[:, p::16], T.Xa[:], Act.Copy, "Xa", "Xar_a")
+        write_cols(16, T.ccf, "ccf", came)
         act(T.hA[:], P[2][:, 0:L], Act.Identity, "P2 " + CC, "hA", bias=BM, scale=0.4995)
         act(T.r23[:], P[3][:], Act.Relu, "P3", "r23")
         act(T.avg[:], T.hA[:], Act.Relu, "hA " + CC, "avg", bias=BMN)
         if not last:
             options_list()
-        dedupe_b(16)
-        cp(T.ccf[:], T.ccu[:], "ccu", "ccf")
-        onehot(128, 2)
-
-        def came(Rt=Rt, rn=rn):
-            ts(T.au[:, 0:6], Rt[:, 0:24:4], 2048.0, None, Alu.add, None, rn, "au")
-            act(T.Xa[:], Xw.indirect(T.au[:, 0:6]), Act.Copy, "X au", "Xa")
-            for p in range(16):
-                act(T.Xar[:, p::16], T.Xa[:], Act.Copy, "Xa", "Xar_a")
-        write_cols(16, T.ccf, "ccf", came)
         mm(P[0][:, 0:L], T.Id[:], T.r23[:, 0:L], True, False, "Id r23", "P0")
         mm(P[0][:, 0:L], T.Id[:], T.r23[:, L:512], False, False, "Id r23", "P0")
         mm(P[0][:, 0:L], T.Id[:], T.avg[:], False, True, "Id avg", "P0")
@@ -665,11 +764,11 @@ def program(g, core, T0, topo):
         act(T.d2[:, 1024:1536], Xw.indirect(T.c3u[:, 64:96]), Act.Copy, "X c3u", "d22")
         ts(T.e1[:, 0:6], Rt[:, 0:24:4], -3000.0, R2B, Alu.is_lt, Alu.mult, rn + " " + CC, "e1")
         mm(P[1][:], T.Id[:], T.d2[:, 1024:1536], True, False, "Id d22", "P1")
-        mm(P[1][:], T.Idm[:], T.Xar[:, 1024:1536], False, True, "Idm Xar_a", "P1")
+        mm(P[1][:], T.Idm[:], T.Xar[:, 1024:1536], False, True, "Idm Xar_a Xar_v", "P1")
         for u in range(2):
             o = 512 * u
             tt(T.d2[:, o:o + 512], Xw.indirect(T.c3u[:, 32 * u:32 * u + 32]), T.Xar[:, o:o + 512], Alu.subtract,
-               "X c3u Xar_a", "d2%d" % u)
+               "X c3u Xar_a Xar_v", "d2%d" % u)
             act(T.a2[:, o:o + 512], T.d2[:, o:o + 512], Act.Abs, "d2%d" % u, "a2%d" % u)
             if u == 0:
                 act(T.a2[:, 1024:1536], P[1][:], Act.Abs, "P1", "a22")
@@ -679,21 +778,24 @@ def program(g, core, T0, topo):
                 rep(6, 0, CAP, T.b16[:, 0:6], "b16")
         farthest(CAP, 1, ["a20 a21 a22"])
         if not last:
+            for p in range(16):
+                if p < AG:
+                    op("g", lambda p=p: g.affine_select(T.Arep[:, p::16], T.A[:, 0:NX], [[0, NX]], Alu.is_ge, 0.0, 0, 0),
+                       "A", "Areg", c=170 + 2 * NX * CYC)
+                else:
+                    act(T.Arep[:, p::16], T.A[:, 0:NX], Act.Copy, "A", "Arep")
             gate_patterns()
         ts(T.c316[:], T.c3u[:], -2048.0, None, Alu.add, None, "c3u", "c316")
         cp(T.c3f[:], T.c3u[:], "c3u", "c3f")
         tt(T.tt[:, 0:CAP], P[6][:, 0:CAP], T.c316[:], Alu.subtract, "c316 P6", "tt")
         dedupe_b(6)
-        if not last:
-            arep()
-        else:
+        if last:
             ts(T.Yw[:], T.Ff[:], G15, RP1, Alu.is_equal, Alu.mult, "Ff " + CC, "Yw")
             ts(T.Yh[:], T.Ff[:], G15, RP1, Alu.is_equal, Alu.mult, "Ff " + CC, "Yh")
         onehot(CAP, 1)
         write_cols(6, T.c3f, "c3f")
     n16 = 16 - NF32
-    half = n16 // 2
-    for a, b, nm in ((0, half, "Ih0"), (half, n16, "Ih1")):
+    for a, b, nm in [(a, min(a + 3, n16), "Ih%d" % (a // 3)) for a in range(0, n16, 3)]:
         ts(T.Ih[:, 256 * a:256 * b], T.It[:, 256 * (NF32 + a):256 * (NF32 + b)], -2048.0, None, Alu.add, None, "It", nm)
     for s in range(16):
         if s < NF32:
@@ -701,8 +803,8 @@ def program(g, core, T0, topo):
         else:
             a = s - NF32
             mm(P[1][:, 256:512], T.Yh[:, 15 - s:143 - s], T.Ih[:, 256 * a:256 * a + 256], False, s == 15,
-               "Yh " + ("Ih0" if a < half else "Ih1"), "P1")
+               "Yh Ih%d" % (a // 3), "P1")
     ts(T.yco[:], P[1][:, 256:512], YB, None, Alu.add, None, "P1 " + CC, "yco")
     dma("s", T.yc[:], T.yco[:], "yco", "out2")
     op("s", lambda: None, "out0 out1 out2 sent", "")
-    schedule(g, T, ops)
+    schedule(g, T, reorder(ops))

from concourse.bass import DstId, RemoteDMATransfer
from concourse.mybir import dt, AluOpType, AxisListType, ActivationFunctionType

W, L, RO, CAP = 4096, 256, 3, 96
NX = 96
NV2 = 1
HOOKQ = 15
RB = (2, 3, 6, 7)
NF32 = 4
XV, AG = 8, 16
PARTS = {"Areg", "c_", "Bc", "Arep", "Rs", "Xcr", "CK", "C16", "OH", "Xar_a", "Xar_v", "d2o"}
CYC, PCYC, VFIX, AFIX, HOP, SELF, LOOK = 0.92, 0.47, 30.0, 50.0, 150.0, 70.0, 60.0
F32, BF, F16, I32, U16 = "float32", "bfloat16", "float16", "int32", "uint16"
IW = W + 32

SCRATCH = {}


def _sb(dtype, **kw):
    for k, n in kw.items():
        SCRATCH[k] = ("sbuf", [128, n], dtype)


_sb(I32, ic=W, TB=W, gi0=16, gi1=16, thi=4, smi=128)
_sb(F32, It=IW, Ff=144, FK=128, Gm=128, col=16, rowm=16, thf=4, thc=4, E8=128, Yw=144, smf=272,
    d10=L, ccf=L, tA=64, OL=48, Nn=48, d2o=32, x2=32,
    Zt=L, Wp=1536, Tt=192, S0=24, S1=24, S2=24, R0=24, R1=24, R2=24,
    Bt=L, base=16, dd2=16, dup=16, SD=L, SC=L, tt=L, tu=L, e1=16, e2=16,
    hA=L, yao=L, ygo=L, yco=L, c3f=CAP)
_sb(BF, X=W, A=L, nA=L, Arep=16 * NX, Xc=L, Xcr=W, dd=48 * NX, rr=48 * NX, ab=48 * (L - NX), d2=W, a2=W,
    Bc=2048, Dm=2048, Sa=144, Sb=144, Sm=144, Rs=432, Q=144, Id=128, Id2=128, Idm=128, BO=128, Uu=128, Tm=128,
    Rk=128, On=128, W16=8, TBK=L, rst=L, RS=L, c75=16, Yh=144, NR0=192, NR1=192, EQ=2048, e2b=64,
    LN=32, LB=32, Pq=16, OH=L, dA=L, r23=512, avg=L, Xa=CAP, Xar=16 * CAP)
_sb(F16, OPT=L, C16=768, cc16=L, A8a=512, A8b=512, FN=768, FS=512, AM=32, dumx=16, b16=16, key=16, g16=16,
    c316=CAP, Ih=W - 256 * NF32)
_sb(U16, gu=16, clu=64, CU=1024, CK=768, ccu=L, offu=16, ou=32, mou=16, au=16, c3u=CAP)
for _k in range(8):
    SCRATCH["P%d" % _k] = ("psum", [128, 512], F32)

NDMA = 24
SEMAPHORES = ["sv", "sa", "sp", "sg"] + ["d%d" % k for k in range(NDMA)] + ["arr0", "arr1", "arr2", "snt"]

Alu = AluOpType
Act = ActivationFunctionType


def schedule(g, T, ops):
    queue = {"v": g.vector, "a": g.scalar, "p": g.tensor, "g": g, "s": g.sync}
    lastw, readers = {}, {}
    known = {e: {} for e in queue}
    waits, clock, needed = [], [], set()
    for i, o in enumerate(ops):
        e, asyn = o["e"], o["sem"] is not None
        deps = set()
        for r in o["r"]:
            if r in lastw:
                deps.add(lastw[r])
        for r in o["w"]:
            prev = list(readers.get(r, [])) + ([lastw[r]] if r in lastw else [])
            for j in prev:
                same = ops[j]["e"] == e and ops[j]["sem"] is None and not asyn
                part = j == lastw.get(r) and (r in PARTS or r.startswith("ab"))
                if j != i and (not same or (e != "p" and not (r[0] == "P" and r[1:].isdigit()) and not part)):
                    deps.add(j)
        w = []
        if o["f"] is not None:
            for j in sorted(deps, reverse=True):
                chan = ops[j]["sem"] or ops[j]["e"]
                if known[e].get(chan, -1) >= j:
                    continue
                w.append(j)
                needed.add(j)
                for c, v in clock[j].items():
                    if known[e].get(c, -1) < v:
                        known[e][c] = v
        waits.append(w)
        ck = dict(known[e]) if o["f"] is not None else {}
        ck[o["sem"] or e] = i
        clock.append(ck)
        for r in o["r"]:
            readers.setdefault(r, []).append(i)
        for r in o["w"]:
            lastw[r] = i
            readers[r] = []
    count, val = {}, {}
    for i, o in enumerate(ops):
        q = queue[o["e"]]
        for j in waits[i]:
            q.wait_ge(T.sem[val[j][0]], val[j][1])
        if o["sem"] is not None:
            count[o["sem"]] = count.get(o["sem"], 0) + o["n"]
            val[i] = (o["sem"], count[o["sem"]])
            if o["f"] is not None:
                ins = o["f"]()
                if o["inc"]:
                    ins.then_inc(T.sem[o["sem"]], o["n"])
        else:
            ins = o["f"]()
            if i in needed:
                s = "s" + o["e"]
                count[s] = count.get(s, 0) + 1
                val[i] = (s, count[s])
                ins.then_inc(T.sem[s], 1)


def reorder(ops):
    n = len(ops)
    lastw, readers, lastq = {}, {}, {}
    pre = []
    for i, o in enumerate(ops):
        d = set(lastw[r] for r in o["r"] if r in lastw)
        for r in o["w"]:
            d.update(readers.get(r, []))
            if r in lastw:
                d.add(lastw[r])
        if o["e"] in "gs" or o["sem"] is not None:
            if o["e"] in lastq:
                d.add(lastq[o["e"]])
            lastq[o["e"]] = i
        d.discard(i)
        pre.append(d)
        for r in o["r"]:
            readers.setdefault(r, []).append(i)
        for r in o["w"]:
            lastw[r] = i
            readers[r] = []

    def gap(j, i):
        a, b = ops[j], ops[i]
        if a["sem"] is not None:
            return a["lat"] if set(a["w"]) & set(b["r"]) or b["f"] is None else 0
        if a["e"] != b["e"]:
            return HOP
        return SELF if set(a["w"]) & set(b["r"]) or (a["e"] == "v" and "It" in b["w"]) else 0

    succ = [[] for _ in ops]
    for i in range(n):
        for j in pre[i]:
            succ[j].append((i, gap(j, i)))
    way = [0.0] * n
    for i in reversed(range(n)):
        way[i] = ops[i]["c"] + max([x + way[k] for k, x in succ[i]] + [0])
    left = [len(p) for p in pre]
    ready = {e: [] for e in "vapgs"}
    at = [0.0] * n
    for i in range(n):
        if not left[i]:
            ready[ops[i]["e"]].append(i)
    free = {e: 0.0 for e in ready}
    order = []
    while len(order) < n:
        best = None
        for e in ready:
            if ready[e]:
                t0 = max(free[e], min(at[i] for i in ready[e]))
                if best is None or t0 < best[0]:
                    best = (t0, e)
        t0, e = best
        i = max((k for k in ready[e] if at[k] <= t0 + LOOK), key=lambda k: (way[k], -k))
        ready[e].remove(i)
        st = max(t0, at[i])
        free[e] = st + ops[i]["c"]
        order.append(i)
        for k, x in succ[i]:
            at[k] = max(at[k], free[e] + x)
            left[k] -= 1
            if not left[k]:
                ready[ops[k]["e"]].append(k)
    return [ops[i] for i in order]


def rank_program(g, core, T, topo):
    if T.rank_of(core) is not None:
        program(g, core, T, topo)


def program(g, core, T0, topo):
    def sf(j):
        return [T0.smf[:, 16 * j:16 * j + 16]]

    def si(j, n=16):
        return [T0.smi[:, 16 * j:16 * j + n]]

    class T:
        icol, pat, alt, gate, acc0, th, yc, ya, yg = T0.icol, T0.pat, T0.alt, T0.gate, T0.acc0, T0.th, T0.yc, T0.ya, T0.yg
        sem, cores = T0.sem, T0.cores
        kc, ri, pi, mi, t1, mc, sh, gs = si(0, 1), si(1, 1), si(2, 1), si(3), si(4), si(5), si(6), si(7)
        (Dl, la, lb, one, two, none1, mdef, pre, hh, ww, t2, yy, offf, cm, ddm, c37, c37e) = [sf(j) for j in range(17)]
        (ic, TB, gi0, thi, It, Ff, FK, Gm, col, rowm, thf, thc, E8, Yw, d10, ccf, tA, OL, Nn, d2o, x2, Zt, Wp, Tt, Bt, base,
         dd2, dup, SD, SC, tt, tu, e1, e2, hA, yao, ygo, yco, c3f) = [T0[k] for k in (
             "ic TB gi0 thi It Ff FK Gm col rowm thf thc E8 Yw d10 ccf tA OL Nn d2o x2 Zt Wp Tt Bt base "
             "dd2 dup SD SC tt tu e1 e2 hA yao ygo yco c3f").split()]
        (X, A, nA, Arep, Xc, Xcr, dd, rr, ab, d2, a2, Bc, Dm, Sa, Sb, Sm, Rs, Q, Id, Id2, Idm, BO, Uu, Tm, Rk, On, W16,
         TBK, rst, RS, c75, Yh, e2b, LN, LB, Pq, OH, dA, r23, avg, Xa, Xar) = [T0[k] for k in (
             "X A nA Arep Xc Xcr dd rr ab d2 a2 Bc Dm Sa Sb Sm Rs Q Id Id2 Idm BO Uu Tm Rk On W16 "
             "TBK rst RS c75 Yh e2b LN LB Pq OH dA r23 avg Xa Xar").split()]
        (OPT, C16, cc16, A8a, A8b, FN, FS, AM, dumx, b16, key, g16, c316, Ih, gu, clu, CU, CK, ccu, offu, ou, mou, au,
         c3u) = [T0[k] for k in ("OPT C16 cc16 A8a A8b FN FS AM dumx b16 key g16 c316 Ih gu clu CU CK ccu offu ou mou au "
                                 "c3u").split()]

    rank = T0.rank_of(core)
    N = len(T.cores)
    ops = []
    nd = [0]
    V, S, PE = g.vector, g.scalar, g.tensor

    def names(x):
        return x.split() if isinstance(x, str) else list(x)

    def un(x):
        return x[0] if isinstance(x, list) else x

    def op(e, f, r, w, sem=None, n=0, inc=False, c=300.0, lat=0.0):
        r, w = names(r), names(w)
        banks = [x for x in r if x[0] == "P" and x[1:].isdigit()]
        ops.append({"e": e, "f": f, "r": [x for x in r if x not in banks], "w": w + banks, "sem": sem, "n": n, "inc": inc,
                    "c": c, "lat": lat})

    def dma(e, out, in_, r, w, lat=2500.0):
        q = {"s": g.sync, "a": g.scalar}[e]
        op(e, lambda: q.dma_start(out, in_), r, w, sem="d%d" % nd[0], n=16, inc=True, c=100.0, lat=lat)
        nd[0] += 1

    def wide(x):
        return "16" not in str(un(x).dtype)

    def cost(out, ins, r, two=1.0, fix=VFIX):
        r = set(names(r))
        if r & {"ou", "offu"}:
            return 50 + un(ins[0]).shape[1] * 3.8 * CYC
        n = un(out).shape[1]
        if r & {"X", "It", "TB0"} and r & {"gu", "clu", "CK", "CUa", "ccu", "c3u", "au", "mou"}:
            return 60 + n * 1.56 * CYC
        if any(x[0] == "P" and x[1:].isdigit() for x in r):
            two = 1.0
        elif not any(wide(x) for x in [out] + ins):
            two *= 0.5
        return fix + max(32, n * two) * CYC

    def ts(out, in0, s1, s2, o0, o1, r, w):
        c = cost(out, [in0], r)
        if o1 is None:
            op("v", lambda: V.tensor_scalar(un(out), un(in0), s1, None, o0), r, w, c=c)
        else:
            op("v", lambda: V.tensor_scalar(un(out), un(in0), s1, s2, o0, o1), r, w, c=c)

    def tt(out, a, b, o, r, w):
        op("v", lambda: V.tensor_tensor(un(out), un(a), un(b), o), r, w, c=cost(out, [a, b], r, 2.0))

    def cp(out, a, r, w):
        op("v", lambda: V.tensor_copy(un(out), un(a)), r, w, c=cost(out, [a], r))

    def ms(out, c, w):
        op("v", lambda: V.memset(out, c), "", w, c=cost(out, [], ""))

    def mm(out, l, rh, st, sp, r, w):
        c = max(min(64, l.shape[1]), rh.shape[1]) * (4 if wide(rh) else 1) * PCYC
        op("p", lambda: PE.matmul(out, l, rh, st, sp), r, w, c=c)

    def act(out, in_, fn, r, w, bias=None, scale=None):
        kw = {}
        if bias is not None:
            kw["bias"] = bias
        if scale is not None:
            kw["scale"] = scale
        op("a", lambda: S.activation(out, in_, fn, **kw), r, w, c=cost(out, [T.It[:]], r, 1.0, AFIX))

    def iota(out, pat, base, cm, w, small=True):
        if small:
            op("g", lambda: g.iota(out, pat, base, cm, allow_small_or_imprecise_dtypes=True), "", w)
        else:
            op("g", lambda: g.iota(un(out), pat, base, cm), "", w)

    P = [T0["P%d" % k] for k in range(8)]
    Xw, Iw = T.X[:, 0:W], T.It[:, 0:IW]
    col = T.col
    RF, G16, G15, K12, RLT3, RP1, R256, PAR, M8, A8C, R2A, R2B, YB, K16, BM, BMN = [col[:, j:j + 1] for j in range(16)]
    MAGIC = 12582912.0
    MAG16 = 201326592.0

    ms(T.TB[:], 0, "TB0")
    dma("a", T.gi0[:], T.gate[:], "", "gi0")
    dma("a", T.thi[0:8, 0:3], T.th[:], "", "thi")
    dma("a", T.A[:], T.acc0[:], "", "A")
    for j in range(4):
        dma("s", T.ic[:, 1024 * j:1024 * j + 1024], T.icol[:, 1024 * j:1024 * j + 1024], "", "ic%d" % j, 3500.0 + 2000 * j)
    for u in range(8):
        dma("s", T.TB[16 * u:16 * u + 3, :], T.alt[3 * u:3 * u + 3, :], "TB0", "TB_%d" % u, 7000.0)
    dma("s", T.X[:], T.pat[:], "", "X", 10500.0)
    TBall = "TB0 " + " ".join("TB_%d" % u for u in range(8))

    iota(T.kc[:], [[0, 1]], 0, 1, "kc", small=False)
    iota(T.Ff[:], [[1, 144]], 0, 0, "Ff")
    iota(T.Gm[:], [[16, 8], [0, 16]], 0, 0, "Gm")
    iota(T.FK[:], [[1, 128]], 0, -1, "FK")
    iota(T.TBK[:], [[0, 16], [-1, 16]], 15, 0, "TBK")
    ts(T.ri[:], T.kc[:], 15, None, Alu.bitwise_and, None, "kc", "ri")
    ts(T.pi[:], T.kc[:], 16, None, Alu.bitwise_and, None, "kc", "pi")
    cp(RF, T.ri[:], "ri", "RF")
    tt(G16, T.kc[:], T.ri[:], Alu.subtract, "kc ri", "G16")
    ts(K12, T.kc[:], 12.0, None, Alu.add, None, "kc", "c_")
    ts(K16, T.kc[:], 16.0, None, Alu.mult, None, "kc", "c_")
    ts(RLT3, T.ri[:], 2.5, None, Alu.is_lt, None, "ri", "c_")
    ts(RP1, T.ri[:], 1.0, None, Alu.add, None, "ri", "c_")
    ts(R256, T.ri[:], 256.0, None, Alu.add, None, "ri", "c_")
    ts(PAR, T.pi[:], 7.5, None, Alu.add, None, "pi", "c_")
    ts(M8, T.ri[:], 8.0, None, Alu.is_equal, None, "ri", "M8")
    ts(R2A, T.ri[:], 2.0, 2048.0, Alu.mult, Alu.add, "ri", "c_")
    ts(R2B, T.ri[:], 2.0, 6144.0, Alu.mult, Alu.add, "ri", "c_")
    ts(YB, T.ri[:], NF32 - 0.5, 2048.0 * 136, Alu.is_gt, Alu.mult, "ri", "c_")
    ms(BM, MAGIC, "c_")
    ms(BMN, -MAGIC, "c_")
    ts(G15, G16, 15.0, None, Alu.add, None, "G16", "c_")
    ts(A8C, M8, 12288.0, -4096.0, Alu.mult, Alu.add, "M8", "c_")
    CC = "c_ RF G16 M8"
    ts(T.rowm[:], T.Ff[:, 0:16], RF, None, Alu.is_equal, None, "Ff " + CC, "rowm")
    ts(T.BO[:], T.Gm[:], G16, None, Alu.is_equal, None, "Gm " + CC, "BO")
    ts(T.Q[:], T.Ff[:], K12, RLT3, Alu.is_equal, Alu.mult, "Ff " + CC, "Q")
    cp(T.gu[:], T.gi0[:], "gi0", "gu")
    for s in range(16):
        act(T.Bc[:, 128 * s:128 * s + 128], T.BO[:], Act.Identity, "BO rowm", "Bc", scale=T.rowm[:, s:s + 1])
    op("g", lambda: g.affine_select(T.Dm[:], T.Bc[:], [[0, 16], [-16, 8], [-1, 16]], Alu.not_equal, -1.0, 0, 1), "Bc", "Dm",
       c=3900.0)
    op("g", lambda: g.affine_select(T.Dm[:], T.Dm[:], [[-1, 16], [0, 8], [1, 16]], Alu.is_gt, 0.0, 0, 0), "Dm", "Dm", c=3900.0)
    act(T.nA[:, NX:L], T.A[:, NX:L], Act.Identity, "A", "nA", scale=-1.0)

    def arep():
        for p in range(16):
            act(T.Arep[:, p::16], T.A[:, 0:NX], Act.Copy, "A", "Arep")
    arep()
    cp(T.It[:, 0:1024], T.ic[:, 0:1024], "ic0", "It")
    ts(T.Sa[:], T.Ff[:], G15, None, Alu.is_equal, None, "Ff " + CC, "Sa")
    ts(T.Sb[:], T.Ff[:], G15, 2.0, Alu.is_equal, Alu.mult, "Ff " + CC, "Sb")
    ts(T.Sm[:], T.Ff[:], G15, -1.0, Alu.is_equal, Alu.mult, "Ff " + CC, "Sm")
    for k in range(3):
        ts(T.Rs[:, 144 * k:144 * k + 144], T.Ff[:], G15, T.rowm[:, k:k + 1], Alu.is_equal, Alu.mult, "Ff rowm " + CC, "Rs")
    ts(T.Id[:], T.FK[:], 0.0, None, Alu.is_equal, None, "FK", "Id")
    ms(T.It[:, W:IW], 0.0, "It")
    cp(T.It[:, 1024:2048], T.ic[:, 1024:2048], "ic1", "It")
    ts(T.Id2[:], T.FK[:], 0.0, 2.0, Alu.is_equal, Alu.mult, "FK", "Id2")
    ts(T.Idm[:], T.FK[:], 0.0, -1.0, Alu.is_equal, Alu.mult, "FK", "Idm")
    ts(T.Uu[:], T.FK[:], 0.0, None, Alu.is_gt, None, "FK", "Uu")
    ts(T.E8[0:8, :], T.Gm[0:8, :], col[0:8, 13:14], None, Alu.is_equal, None, "Gm " + CC, "E8")
    cp(T.thf[0:8, 0:3], T.thi[0:8, 0:3], "thi", "thf")
    tt(T.Uu[:], T.Uu[:], T.BO[:], Alu.mult, "Uu BO", "Uu")
    mm(P[0][:, 0:3], T.E8[0:8, :], T.thf[0:8, 0:3], True, True, "E8 thf", "P0")
    ts(T.W16[:], T.Gm[:, 0::16], G16, 16.0, Alu.is_equal, Alu.mult, "Gm " + CC, "W16")
    tt(T.Tm[:], T.Id[:], T.Uu[:], Alu.subtract, "Id Uu", "Tm")
    tt(T.Rk[:], T.Uu[:], T.BO[:], Alu.subtract, "Uu BO", "Rk")
    cp(T.It[:, 2048:3072], T.ic[:, 2048:3072], "ic2", "It")
    ts(T.Tm[:], T.Tm[:], 8192.0, None, Alu.mult, None, "Tm", "Tm")
    cp(T.thc[:, 0:3], P[0][:, 0:3], "P0", "thc")
    ms(T.On[:], 1.0, "On")
    ms(T.c75[:], -7.5, "c75")
    ts(T.rst[:], T.TBK[:], 15.0, None, Alu.not_equal, None, "TBK", "rst")
    ts(T.RS[:], T.TBK[:], RF, None, Alu.is_ge, None, "TBK " + CC, "RS")
    ts(T.Dl[:], T.Ff[:, 0:16], 16.0, R256, Alu.mult, Alu.add, "Ff " + CC, "Dl")
    for t in range(RO):
        ms(T0["S%d" % t][:], 0.0, "S%d" % t)
    cp(T.It[:, 3072:4096], T.ic[:, 3072:4096], "ic3", "It")

    def rep(out_bank, c0, n, rhs, r):
        for s in range(16):
            mm(P[out_bank][:, c0 + s:c0 + n:16], T.Bc[:, 128 * s:128 * s + 128], rhs, True, True, "Bc " + r, "P%d" % out_bank)

    def options_first():
        ts(T.OPT[:], T.TB[:, 0:W].indirect(T.gu[:]), -2048.0, None, Alu.add, None, TBall + " gu", "OPT")
        for u in range(4):
            mm(P[5][:, 0:64], T.Q[:, 12 - 4 * u:140 - 4 * u], T.OPT[:, u::4], u == 0, u == 3, "Q OPT", "P5")

    def options_list():
        ts(T.clu[:], P[5][:, 0:64], 2048.0, None, Alu.add, None, "P5", "clu")

    def options_turn():
        for k in range(3):
            for s in range(16):
                mm(P[5][:, 64 + 16 * k:80 + 16 * k], T.Rs[:, 144 * k + 15 - s:144 * k + 143 - s], T.OPT[:, s::16],
                   s == 0, s == 15, "Rs OPT", "P5")

    def options_rest(gi, gn):
        ts(T.t1[:], gi[:], 1, None, Alu.bitwise_and, None, gn, "t1")
        ts(T.cm[:], gi[:], -2048.0, None, Alu.add, None, gn, "cm")
        ts(T.t2[:], T.t1[:], -2.0, 1.0, Alu.mult, Alu.add, "t1", "t2")
        ts(T.c37[:], gi[:], 37.0, None, Alu.mult, None, gn, "c37")
        tt(T.b16[:], T.t2[:], T.cm[:], Alu.add, "t2 cm", "b16")
        ts(T.ddm[:], T.cm[:], -1.0, R2A, Alu.mult, Alu.add, "cm " + CC, "ddm")
        cp(T.OL[:], P[5][:, 64:112], "P5", "OL")
        rep(6, 0, L, T.b16[:], "b16")
        tt(T.d2o[:, 0:16], T.OL[:, 0:16], T.OL[:, 32:48], Alu.subtract, "OL", "d2o")
        tt(T.d2o[:, 16:32], T.OL[:, 16:32], T.OL[:, 32:48], Alu.subtract, "OL", "d2o")
        ms(T.Wp[:, 0:192], -4096.0, "Wp")
        ts(T.Bt[:], P[6][:, 0:L], M8, A8C, Alu.mult, Alu.add, "P6 " + CC, "Bt")

    def gate_patterns():
        act(T.Xc[:], Xw.indirect(T.gu[:]), Act.Copy, "X gu", "Xc")
        for p in range(16):
            op("g", lambda p=p: g.affine_select(T.Xcr[:, p::16], T.Xc[:], [[0, L]], Alu.is_ge, 0.0, 0, 0), "Xc", "Xcr", c=650.0)

    def segs(c):
        lo, hi = 64 * c, 64 * c + 64
        out = []
        if lo < NX:
            out.append(("v", lo, min(hi, NX) - lo, 0))
        if hi > NX:
            a = max(lo, NX)
            if c == 3 and hi - a == 64:
                out += [("a", a, 32, 0), ("a", a + 32, 32, 96)]
            else:
                out.append(("a", a, hi - a, 3 * (a - lo)))
        return out

    def t1v(c, k):
        e, lo, n, c0 = segs(c)[0]
        if e != "v":
            return
        o = 48 * lo + 16 * n * k
        nm = "dd%d%d" % (c, k)
        tt(T.dd[:, o:o + 16 * n], Xw.indirect(T.CK[:, 256 * k + lo:256 * k + lo + n]), T.Arep[:, 16 * lo:16 * (lo + n)],
           Alu.subtract, "X CK Arep Areg", nm)
        ts(T.rr[:, o:o + 16 * n], T.dd[:, o:o + 16 * n], 0.0, None, Alu.max, None, nm, "r" + nm)
        b = c % 2
        for p in range(16):
            mm(P[b][:, n * k:n * k + n], T.Sm[:, 15 - p:143 - p], T.dd[:, o + p:o + 16 * n:16], p == 0, False, "Sm " + nm, "P%d" % b)
        for p in range(16):
            mm(P[b][:, n * k:n * k + n], T.Sb[:, 15 - p:143 - p], T.rr[:, o + p:o + 16 * n:16], False, p == 15, "Sb r" + nm, "P%d" % b)

    def t1a(lo, n):
        for l in range(lo, lo + n):
            o = 48 * (l - NX)
            act(T.ab[:, o:o + 48], Xw.indirect(T.CU[:, 4 * l:4 * l + 3]), Act.Abs, "X CUa nA", "abq ab%d" % lo, bias=T.nA[:, l:l + 1])

    def suma(c, lo, n, c0):
        o = 48 * (lo - NX)
        b = c % 2
        for p in range(16):
            mm(P[b][:, c0:c0 + 3 * n], T.Sa[:, 15 - p:143 - p], T.ab[:, o + p:o + 48 * n:16], p == 0, p == 15, "Sa ab%d" % lo, "P%d" % b)

    def near(c, t):
        b = c % 2
        NR = T0["NR%d" % b]
        ts(NR[:], P[b][:, 0:192], T.thc[:, t:t + 1], None, Alu.is_le, None, "thc P%d" % b, "NR%d" % b)
        for e, lo, n, c0 in segs(c):
            for k in range(3):
                rhs = NR[:, c0 + n * k:c0 + n * k + n] if e == "v" else NR[:, c0 + k:c0 + 3 * n:3]
                o = 256 + 64 * k + lo - 64 * c
                mm(P[b][:, o:o + n], T.BO[:], rhs, True, True, "BO NR%d" % b, "P%d" % b)

    def rot(c, j):
        b = RB[j]
        for i in range(4):
            s = 4 * j + i
            for h in range(2):
                mm(P[b][:, 128 * i + 64 * h:128 * i + 64 * h + 64], T.Bc[:, 128 * s:128 * s + 128],
                   T.C16[:, 256 * (h + 1) + 64 * c:256 * (h + 1) + 64 * c + 64], True, True, "Bc C16", "P%d" % b)

    def first_col(c):
        b = c % 2
        A8, an = (T.A8a, "A8a") if b == 0 else (T.A8b, "A8b")
        lo = 64 * c
        for k in range(3):
            ts(T.FN[:, 256 * k + lo:256 * k + lo + 64], P[b][:, 256 + 64 * k:320 + 64 * k], 7.5, None, Alu.is_lt, None,
               "P%d" % b, "FN%d%d" % (c, k))
        tt(T.tA[:], T.FN[:, lo:lo + 64], T.d10[:, lo:lo + 64], Alu.mult, "d10 FN%d0" % c, "tA")
        tt(A8[:, 0:64], T.tA[:], T.C16[:, lo:lo + 64], Alu.add, "tA C16", an)
        for n in (64, 128, 256):
            cp(A8[:, n:2 * n], A8[:, 0:n], an, an)

    def member(c, after={}):
        b = c % 2
        A8, an = (T.A8a, "A8a") if b == 0 else (T.A8b, "A8b")
        for j in range(4):
            o = 512 * j
            tt(T0.EQ[:, o:o + 512], A8[:], P[RB[j]][:], Alu.is_equal, an + " P%d" % RB[j], "EQ%d" % j)
            for i in range(4):
                mm(P[4][:, 0:128], T.Id[:], T0.EQ[:, o + 128 * i:o + 128 * i + 128], j == 0 and i == 0, j == 3 and i == 3,
                   "Id EQ%d" % j, "P4")
            if j == 0:
                for h in range(2):
                    o = 256 * (h + 1) + 64 * c
                    mm(P[4][:, 64 * h:64 * h + 64], T.Id[:], T.FN[:, o:o + 64], False, False, "Id FN%d%d" % (c, h + 1), "P4")
            if c < 3 and j < 2:
                rot(c + 1, j)
            if j in after:
                after[j]()
        if c < 3:
            late.append(c + 1)

    def okrows(c):
        b = c % 2
        A8, an = (T.A8a, "A8a") if b == 0 else (T.A8b, "A8b")
        o = 256 + 64 * c
        ts(T.e2b[:], P[4][:, 64:128], 1.0, None, Alu.min, None, "P4", "e2b")
        tt(T.FS[:, o:o + 64], T.e2b[:], P[4][:, 0:64], Alu.min, "e2b P4", "FSo%d" % c)
        mm(P[4][:, 256:320], T.Id[:], A8[:, 0:64], True, False, "Id " + an, "P4")
        mm(P[4][:, 256:320], T.Tm[:], T.FS[:, o:o + 64], False, True, "Tm FSo%d" % c, "P4")
        if late:
            c1 = late.pop()
            rot(c1, 2)
            rot(c1, 3)

    def selrow(c):
        ts(T.FS[:, 64 * c:64 * c + 64], P[4][:, 256:320], -8192.0, -2048.0, Alu.add, Alu.max, "P4", "FSs%d" % c)

    def s2gather(u):
        o = 1024 * u
        tt(T.d2[:, o:o + 1024], Xw.indirect(T.ccu[:, 64 * u:64 * u + 64]), T.Xcr[:, o:o + 1024], Alu.subtract, "X ccu Xcr",
           "d2%d d2%d" % (2 * u, 2 * u + 1))

    def s2abs(u):
        o = 1024 * u
        act(T.a2[:, o:o + 1024], T.d2[:, o:o + 1024], Act.Abs, "d2%d d2%d" % (2 * u, 2 * u + 1), "a2%d a2%d" % (2 * u, 2 * u + 1))

    def s2fetch(i):
        if i < 8:
            act(T.d2[:, 512 * i:512 * i + 512], Xw.indirect(T.ccu[:, 32 * i:32 * i + 32]), Act.Copy, "X ccu", "d2%d" % i)

    def s2piece(i):
        o = 512 * i
        mm(P[0][:], T.Id[:], T.d2[:, o:o + 512], True, False, "Id d2%d" % i, "P0")
        mm(P[0][:], T.Idm[:], T.Xcr[:, o:o + 512], False, True, "Idm Xcr", "P0")
        s2fetch(i + 1)
        act(T.a2[:, o:o + 512], P[0][:], Act.Abs, "P0", "a2%d" % i)

    late = []

    def farthest(n, halves, r):
        w = 128 * halves
        mm(P[7][0:n, 0:w], T.Id[:, 0:n], T.TBK[:, 0:w], True, False, "Id TBK", "P7")
        for h in range(halves):
            for p in range(16):
                mm(P[7][0:n, 128 * h + p:128 * h + 128:16], T.a2[:, 2048 * h + p:2048 * h + 16 * n:16], T.W16[:], False,
                   h == halves - 1 and p == 15, "W16 " + r[h], "P7")

    def onehot(n, halves, on_scalar=False):
        w = 128 * halves
        op("v", lambda: V.tensor_tensor_scan(T.SC[0:n, 0:w], T.rst[0:n, 0:w], P[7][0:n, 0:w], 0.0, Alu.mult, Alu.max), "rst P7", "SC")
        if on_scalar:
            ts(T.x2[:, 0:16], T.SC[:, 15:w:16], -1.0, 1.0, Alu.mult, Alu.add, "SC", "x2")
            for u in range(8 * halves):
                act(T.OH[:, 16 * u:16 * u + 16], P[7][:, 16 * u:16 * u + 16], Act.Relu, "x2 P7", "OH", bias=T.x2[:, u:u + 1])
        for u in range(0 if on_scalar else 8 * halves):
            ts(T.OH[0:n, 16 * u:16 * u + 16], P[7][0:n, 16 * u:16 * u + 16], T.SC[0:n, 16 * u + 15:16 * u + 16], None,
               Alu.is_equal, None, "SC P7", "OH")
        for h in range(halves):
            mm(P[7][:, 256 + 128 * h:256 + 128 * h + n], T.OH[0:n, 128 * h:128 * h + 128], T.Id[0:n, 0:n], True, True, "OH Id", "P7")

    def dedupe_a(nq):
        ts(T.key[:, 0:nq], T.base[:, 0:nq], 1.0 / 64, None, Alu.mult, None, "base", "key")
        for s in range(16):
            mm(P[4][:, 15 - s:16 * nq:16], T.Dm[:, 128 * s:128 * s + 128], T.key[:, 0:nq], True, True, "Dm key", "P4")
        ts(T.dd2[:, 0:nq], T.base[:, 0:nq], -1.0, R2A, Alu.mult, Alu.add, "base " + CC, "dd2")

    def dedupe_b(nq):
        w = 16 * nq
        op("v", lambda: V.tensor_tensor_scan(T.SD[:, 0:w], P[4][:, 0:w], T.RS[:, 0:w], 1.0, Alu.mult, Alu.add), "RS P4", "SD")
        ts(T.dup[:, 0:nq], T.SD[:, 15:w:16], 0.0, None, Alu.is_equal, None, "SD", "dup")
        tt(T.e1[:, 0:nq], T.dup[:, 0:nq], T.dd2[:, 0:nq], Alu.mult, "dup dd2", "e1")
        tt(T.e2[:, 0:nq], T.e1[:, 0:nq], T.base[:, 0:nq], Alu.add, "e1 base", "e2")
        ts(T.ou[:, 0:2 * nq:2], T.e2[:, 0:nq], 2048.0, None, Alu.add, None, "e2", "ou")

    def write_cols(nq, cf, cn, hook=None):
        n = 16 * nq
        tt(T.tu[:, 0:n], T.tt[:, 0:n], P[7][:, 256:256 + n], Alu.mult, "tt P7", "tu")
        for q in reversed(range(nq)):
            if hook and q == HOOKQ:
                hook()
            tt(Iw.indirect(T.ou[:, 2 * q:2 * q + 1]), cf[:, 16 * q:16 * q + 16], T.tu[:, 16 * q:16 * q + 16], Alu.add,
               "ou tu " + cn, "It")

    options_first()
    options_list()
    gate_patterns()
    for t in range(RO):
        gi, gn = T0["gi%d" % (t % 2)], "gi%d" % (t % 2)
        gj, gm = T0["gi%d" % ((t + 1) % 2)], "gi%d" % ((t + 1) % 2)
        last = t == RO - 1
        St, sn = T0["S%d" % t], "S%d" % t
        Rt, rn = T0["R%d" % t], "R%d" % t
        cp(T.CU[:, 4 * NX:1024], Iw.indirect(T.clu[:, NX // 4:64]), "It clu", "CUa")
        asegs = [(c, s) for c in range(4) for s in segs(c) if s[0] == "a"]
        for c, s in asegs:
            t1a(s[1], s[2])
        options_turn()
        cp(T.CU[:, 0:4 * NX], Iw.indirect(T.clu[:, 0:NX // 4]), "It clu", "CUv")
        for k in range(3):
            cp(T.CK[:, 256 * k:256 * k + NX], T.CU[:, k:4 * NX:4], "CUv", "CK")
        for k in range(3):
            t1v(0, k)
        options_rest(gi, gn)
        for k in range(3):
            ts(T.C16[:, 256 * k:256 * k + 256], T.CU[:, k::4], -2048.0, None, Alu.add, None, "CUa CUv", "C16")
        tt(T.d10[:], T.C16[:, 256:512], T.C16[:, 0:256], Alu.subtract, "C16", "d10")
        t1v(1, 0)
        near(0, t)
        for j in range(4):
            rot(0, j)
        t1v(1, 1)
        t1v(1, 2)
        for c, s in asegs:
            if c == 1:
                suma(c, s[1], s[2], s[3])
        first_col(0)
        a3 = [s for c, s in asegs if c == 3]
        piece = [2 * NV2]

        def s2next():
            if piece[0] < 8:
                s2piece(piece[0])
                piece[0] += 1
        near(1, t)
        cp(T.ccu[:], Iw.indirect(T.gu[:]), "It gu", "ccu")
        member(0)
        first_col(1)
        for c, s in asegs:
            if c == 2:
                suma(c, s[1], s[2], s[3])
        okrows(0)
        near(2, t)
        selrow(0)
        member(1)
        first_col(2)
        for s in a3[:-1]:
            suma(3, s[1], s[2], s[3])
        okrows(1)
        ts(T.cc16[:], T.ccu[:], -2048.0, None, Alu.add, None, "ccu", "cc16")
        for u in range(NV2):
            s2gather(u)
        selrow(1)
        s2fetch(piece[0])
        act(T.ccf[:], Iw.indirect(T.gu[:]), Act.Copy, "It gu", "ccf")
        member(2, {1: lambda: suma(3, a3[-1][1], a3[-1][2], a3[-1][3]), 2: s2next})
        near(3, t)
        okrows(2)
        s2next()
        first_col(3)
        selrow(2)
        FNall = " ".join("FN%d%d" % (c, k) for c in range(4) for k in range(3))

        def survivors():
            for s in range(16):
                mm(P[5][:, 160:208], T.Sa[:, 15 - s:143 - s], T.FN[:, s::16], s == 0, s == 15, "Sa " + FNall, "P5")
        survivors()
        member(3, {0: s2next})
        ts(T.Nn[:], P[5][:, 160:208], -1.0 / 16, 1.0, Alu.mult, Alu.add, "P5", "Nn")
        okrows(3)
        s2next()
        tt(T.la[:], T.Nn[:, 0:16], T.Nn[:, 16:32], Alu.add, "Nn", "la")
        tt(T.x2[:], T.Nn[:, 0:32], T.d2o[:], Alu.mult, "Nn d2o", "x2")
        tt(T.la[:], T.la[:], T.Nn[:, 32:48], Alu.add, "la Nn", "la")
        selrow(3)
        FSall = " ".join("FS%s%d" % (x, c) for c in range(4) for x in "so")
        for s in range(16):
            mm(P[5][:, 128:160], T.Sa[:, 15 - s:143 - s], T.FS[:, s::16], s == 0, s == 15, "Sa " + FSall, "P5")
        s2next()
        tt(T.lb[:], T.x2[:, 0:16], T.x2[:, 16:32], Alu.add, "x2", "lb")
        ts(T.one[:], T.la[:], 1.0, None, Alu.is_equal, None, "la", "one")
        ts(T.two[:], T.la[:], 1.5, None, Alu.is_gt, None, "la", "two")
        ts(T.none1[:], T.la[:], 1.0, None, Alu.not_equal, None, "la", "none1")
        tt(T.lb[:], T.lb[:], T.one[:], Alu.mult, "lb one", "lb")
        tt(T.mdef[:], T.lb[:], T.OL[:, 32:48], Alu.add, "lb OL", "mdef")
        tt(T.hh[:], T.two[:], P[5][:, 144:160], Alu.min, "two P5", "hh")
        tt(T.LN[:, 16:32], T.hh[:], T.one[:], Alu.add, "hh one", "lrn")
        tt(T.LN[:, 0:16], T.none1[:], T.hh[:], Alu.subtract, "none1 hh", "nl")
        tt(T.pre[:], P[5][:, 128:144], T.mdef[:], Alu.subtract, "mdef P5", "pre")
        op("v", lambda: V.tensor_tensor_scan(T.Pq[:], T.On[:, 0:16], T.LN[:, 16:32], 0.0, Alu.mult, Alu.add), "On lrn", "Pq")
        tt(T.dumx[:], T.LN[:, 0:16], T.Dl[:], Alu.mult, "nl Dl", "dumx")
        ts(T.pre[:], T.pre[:], 30720.0, None, Alu.add, None, "pre", "pre")
        mm(P[5][:, 224:240], T.Id[:], T.c75[:], True, False, "Id c75", "P5")
        mm(P[5][:, 224:240], T.Rk[:], T.LN[:, 16:32], False, False, "Rk lrn", "P5")
        mm(P[5][:, 224:240], T.BO[:], T.Pq[:], False, False, "BO Pq", "P5")
        mm(P[5][:, 224:240], T.Id[:], T.dumx[:], False, True, "Id dumx", "P5")
        mm(P[5][:, 240:241], T.On[:], T.Pq[:, 15:16], True, True, "On Pq", "P5")
        tt(T.ww[:], T.pre[:], T.hh[:], Alu.mult, "pre hh", "ww")
        tt(T.AM[:, 16:32], T.ww[:], T.mdef[:], Alu.add, "ww mdef", "m16")
        ts(T.mi[:], T.AM[:, 16:32], 2048.0, None, Alu.add, None, "m16", "mi")
        ts(T.yy[:], P[5][:, 224:240], MAG16, -MAG16, Alu.add, Alu.add, "P5", "yy")
        ts(T.t1[:], T.mi[:], 1, None, Alu.bitwise_and, None, "mi", "t1")
        tt(T.offf[:], T.yy[:], P[5][:, 224:240], Alu.add, "yy P5", "offf")
        ts(T.t2[:], T.t1[:], -2.0, 1.0, Alu.mult, Alu.add, "t1", "t2")
        ts(T.offu[:], T.offf[:], PAR, None, Alu.add, None, "offf " + CC, "offu")
        tt(T.AM[:, 0:16], T.t2[:], T.AM[:, 16:32], Alu.add, "t2 m16", "a16")
        rep(6, 0, L, T.AM[:, 0:16], "a16")
        for u in range(8):
            s2next()
        for u in range(NV2):
            s2abs(u)
        farthest(128, 2, ["a20 a21 a22 a23", "a24 a25 a26 a27"])
        mm(P[1][:, 0:L], T.Idm[:], T.cc16[:], True, False, "Idm cc16", "P1")
        for s in range(16):
            mm(P[1][:, s:L:16], T.Bc[:, 128 * s:128 * s + 128], T.AM[:, 16:32], False, s == 15, "Bc m16", "P1")
        act(T.LB[:], T.LN[:], Act.Identity, "lrn nl", "LB", scale=-1024.0)
        act(T.tt[:], P[1][:, 0:L], Act.Copy, "P1", "tt")
        ts(T.c37e[:], T.c37[:], P[5][:, 240:241], None, Alu.add, None, "c37 P5", "c37e")
        tt(T.mc[:], T.mi[:], gi[:], Alu.mult, "mi " + gn, "mc")
        tt(T.e1[:], T.LN[:, 0:16], T.ddm[:], Alu.mult, "nl ddm", "e1")
        ts(T.sh[:], T.mc[:], 4, None, Alu.arith_shift_right, None, "mc", "sh")
        tt(T.base[:], T.e1[:], T.cm[:], Alu.add, "e1 cm", "base")
        tt(T.Zt[:], T.Bt[:], P[6][:, 0:L], Alu.max, "Bt P6", "Zt")
        cp(T.Wp[:, 0:1536].indirect(T.offu[:]), T.Zt[:], "offu Zt", "Wp")
        op("v", lambda: V.transpose(T.Tt[:], T.Wp[:, 0:192]), "Wp", "Tt")
        tt(St[:, 0:22], T.Tt[:, 0:176:8], T.Tt[:, 16:192:8], Alu.max, "Tt", sn)
        dst = T.cores[(rank + 1 + t % (N - 1)) % N]
        src = T.cores[(rank - 1 - t % (N - 1)) % N]
        rid, pid = topo.addr(dst)[0], topo.addr(dst)[1]
        eng = topo.engines(core, dst)[::2]
        mask = sum(1 << x for x in eng)
        op("g", lambda St=St, Rt=Rt, t=t, pid=pid, rid=rid, mask=mask:
           g.remote_dma(Rt[:], St[:], T.sem["arr%d" % t], T.sem.snt, pid, rid, mask), sn, "sent", sem="snt", n=len(eng),
           c=500.0, lat=3000.0)
        op("g", None, "", rn, sem="arr%d" % t, n=len(topo.engines(src, core)[::2]), c=0.0)
        dedupe_a(16)
        onehot(128, 2, True)
        tt(T.gs[:], T.sh[:], T.c37e[:], Alu.add, "sh c37e", "gs")
        tt(T.e2[:], T.AM[:, 16:32], T.OL[:, 0:16], Alu.subtract, "m16 OL", "e2")
        ts(gj[:], T.gs[:], W - 1, None, Alu.bitwise_and, None, "gs", gm)
        tt(T.e2[:], T.e2[:], T.LN[:, 16:32], Alu.mult, "e2 lrn", "e2")
        if not last:
            cp(T.gu[:], gj[:], gm, "gu")
        else:
            ts(T.g16[:], gj[:], -2048.0, None, Alu.add, None, gm, "g16")
        tt(T.e2[:], T.e2[:], T.OL[:, 0:16], Alu.add, "e2 OL", "e2")
        ts(T.mou[:], T.e2[:], 2048.0, None, Alu.add, None, "e2", "mou")
        dedupe_b(16)
        if not last:
            options_first()
        act(T.dA[:], Xw.indirect(T.mou[:]), Act.Copy, "X mou", "dA")
        mm(P[2][:, 0:L], T.Id[:], T.dA[:], True, False, "Id dA", "P2")
        mm(P[2][:, 0:L], T.Id[:], T.A[:], False, False, "Id A", "P2")
        for s in range(16):
            mm(P[2][:, s:L:16], T.Bc[:, 128 * s:128 * s + 128], T.LB[:, 0:16], False, s == 15, "Bc LB", "P2")
        for h, (I_, inm) in enumerate(((T.Id, "Id"), (T.Idm, "Idm"))):
            mm(P[3][:, L * h:L * h + L], I_[:], T.dA[:], True, False, inm + " dA", "P3")
            mm(P[3][:, L * h:L * h + L], (T.Idm, T.Id)[h][:], T.A[:], False, False, "Id Idm A", "P3")
            for s in range(16):
                mm(P[3][:, L * h + s:L * h + L:16], T.Bc[:, 128 * s:128 * s + 128], T.LB[:, 16:32], False, s == 15, "Bc LB", "P3")

        def came(Rt=Rt, rn=rn):
            ts(T.au[:, 0:6], Rt[:, 0:24:4], 2048.0, None, Alu.add, None, rn, "au")
            act(T.Xa[:], Xw.indirect(T.au[:, 0:6]), Act.Copy, "X au", "Xa")
            for p in range(XV):
                cp(T.Xar[:, p::16], T.Xa[:], "Xa", "Xar_v")
            for p in range(XV, 16):
                act(T.Xar[:, p::16], T.Xa[:], Act.Copy, "Xa", "Xar_a")
        write_cols(16, T.ccf, "ccf", came)
        act(T.hA[:], P[2][:, 0:L], Act.Identity, "P2 " + CC, "hA", bias=BM, scale=0.4995)
        act(T.r23[:], P[3][:], Act.Relu, "P3", "r23")
        act(T.avg[:], T.hA[:], Act.Relu, "hA " + CC, "avg", bias=BMN)
        if not last:
            options_list()
        mm(P[0][:, 0:L], T.Id[:], T.r23[:, 0:L], True, False, "Id r23", "P0")
        mm(P[0][:, 0:L], T.Id[:], T.r23[:, L:512], False, False, "Id r23", "P0")
        mm(P[0][:, 0:L], T.Id[:], T.avg[:], False, True, "Id avg", "P0")
        if not last:
            act(T.A[:], P[0][:, 0:L], Act.Copy, "P0", "A")
            act(T.nA[:, NX:L], P[0][:, NX:L], Act.Identity, "P0", "nA", scale=-1.0)
        else:
            act(T.yao[:], P[0][:, 0:L], Act.Copy, "P0", "yao")
            dma("s", T.ya[:], T.yao[:], "yao", "out0")
            for s in range(16):
                mm(P[1][0:8, s:L:16], T.Bc[:, 128 * s:128 * s + 128:16], T.g16[:], True, True, "Bc g16", "P1")
            ts(T.ygo[0:8, :], P[1][0:8, 0:L], 2048.0, None, Alu.add, None, "P1", "ygo")
            dma("s", T.yg[:], T.ygo[0:8, :], "ygo", "out1")
        cp(T.c3u[:], Iw.indirect(T.au[:, 0:6]), "It au", "c3u")
        act(T.d2[:, 1024:1536], Xw.indirect(T.c3u[:, 64:96]), Act.Copy, "X c3u", "d22")
        ts(T.e1[:, 0:6], Rt[:, 0:24:4], -3000.0, R2B, Alu.is_lt, Alu.mult, rn + " " + CC, "e1")
        mm(P[1][:], T.Id[:], T.d2[:, 1024:1536], True, False, "Id d22", "P1")
        mm(P[1][:], T.Idm[:], T.Xar[:, 1024:1536], False, True, "Idm Xar_a Xar_v", "P1")
        for u in range(2):
            o = 512 * u
            tt(T.d2[:, o:o + 512], Xw.indirect(T.c3u[:, 32 * u:32 * u + 32]), T.Xar[:, o:o + 512], Alu.subtract,
               "X c3u Xar_a Xar_v", "d2%d" % u)
            act(T.a2[:, o:o + 512], T.d2[:, o:o + 512], Act.Abs, "d2%d" % u, "a2%d" % u)
            if u == 0:
                act(T.a2[:, 1024:1536], P[1][:], Act.Abs, "P1", "a22")
                tt(T.base[:, 0:6], T.e1[:, 0:6], Rt[:, 0:24:4], Alu.add, "e1 " + rn, "base")
                ts(T.b16[:, 0:6], Rt[:, 1:24:4], -8192.0, None, Alu.add, None, rn, "b16")
                dedupe_a(6)
                rep(6, 0, CAP, T.b16[:, 0:6], "b16")
        farthest(CAP, 1, ["a20 a21 a22"])
        if not last:
            for p in range(16):
                if p < AG:
                    op("g", lambda p=p: g.affine_select(T.Arep[:, p::16], T.A[:, 0:NX], [[0, NX]], Alu.is_ge, 0.0, 0, 0),
                       "A", "Areg", c=170 + 2 * NX * CYC)
                else:
                    act(T.Arep[:, p::16], T.A[:, 0:NX], Act.Copy, "A", "Arep")
            gate_patterns()
        ts(T.c316[:], T.c3u[:], -2048.0, None, Alu.add, None, "c3u", "c316")
        cp(T.c3f[:], T.c3u[:], "c3u", "c3f")
        tt(T.tt[:, 0:CAP], P[6][:, 0:CAP], T.c316[:], Alu.subtract, "c316 P6", "tt")
        dedupe_b(6)
        if last:
            ts(T.Yw[:], T.Ff[:], G15, RP1, Alu.is_equal, Alu.mult, "Ff " + CC, "Yw")
            ts(T.Yh[:], T.Ff[:], G15, RP1, Alu.is_equal, Alu.mult, "Ff " + CC, "Yh")
        onehot(CAP, 1)
        write_cols(6, T.c3f, "c3f")
    n16 = 16 - NF32
    for a, b, nm in [(a, min(a + 3, n16), "Ih%d" % (a // 3)) for a in range(0, n16, 3)]:
        ts(T.Ih[:, 256 * a:256 * b], T.It[:, 256 * (NF32 + a):256 * (NF32 + b)], -2048.0, None, Alu.add, None, "It", nm)
    for s in range(16):
        if s < NF32:
            mm(P[1][:, 256:512], T.Yw[:, 15 - s:143 - s], T.It[:, 256 * s:256 * s + 256], s == 0, False, "Yw It", "P1")
        else:
            a = s - NF32
            mm(P[1][:, 256:512], T.Yh[:, 15 - s:143 - s], T.Ih[:, 256 * a:256 * a + 256], False, s == 15,
               "Yh Ih%d" % (a // 3), "P1")
    ts(T.yco[:], P[1][:, 256:512], YB, None, Alu.add, None, "P1 " + CC, "yco")
    dma("s", T.yc[:], T.yco[:], "yco", "out2")
    op("s", lambda: None, "out0 out1 out2 sent", "")
    schedule(g, T, reorder(ops))
